import numpy as np
import ml_dtypes


def mxq(x, axis, fmt="e4m3"):
    dtype, down = {"e4m3": (ml_dtypes.float8_e4m3fn, 7), "e5m2": (ml_dtypes.float8_e5m2, 14)}[fmt]
    v = np.moveaxis(np.asarray(x, np.float32).astype(ml_dtypes.bfloat16).astype(np.float64), axis, -1)
    blocks = v.reshape(v.shape[:-1] + (-1, 32))
    amax = np.abs(blocks).max(-1, keepdims=True)
    byte = np.maximum(np.where(amax > 0, np.frexp(amax)[1] - 1 + 127, 0) - down, 1)
    scale = np.exp2(byte - 127.0)
    codes = (blocks / scale).astype(np.float32).astype(dtype).astype(np.float64)
    return np.moveaxis((codes * scale).reshape(v.shape), -1, axis)


WIDE = False


def mx_kscale(k):
    if not WIDE:
        return np.ones(k)
    levels = np.array([10, -10, 5, -5, 0])
    if k % 512:
        return np.exp2(np.random.permutation(np.resize(levels, k // 32))).repeat(32)
    a = np.empty((k // 512, 16))
    for p in range(k // 512):
        a[p, :8] = np.random.permutation(np.resize(levels, 8))
        for g in range(8):
            far = levels[np.abs(levels - a[p, g]) >= 10]
            a[p, g + 8] = far[np.random.randint(len(far))]
    return np.exp2(a.ravel()).repeat(32)


BF16 = ml_dtypes.bfloat16


def bf(x):
    return np.asarray(x, np.float32).astype(BF16)


def f64(x):
    return np.asarray(x).astype(np.float64)

E4M3FN = np.array([(-1.0 if i & 128 else 1.0) * ((1.0 + (i & 7) / 8.0) * 2.0 ** (((i >> 3) & 15) - 7) if i & 120 else (i & 7) * 2.0 ** -9) for i in range(256)])


def e4m3fn_bytes(y):
    return np.clip(np.asarray(y, np.float64), -448.0, 448.0).astype(np.float32).astype(ml_dtypes.float8_e4m3fn).view(np.uint8)


def e4m3fn_values(b):
    return E4M3FN[b]


M, D, N, R = 1024, 1024, 2048, 1024


def setup_inputs():
    s, t = mx_kscale(D), mx_kscale(N)
    x = np.random.standard_normal((M, D)) * s
    Z = 0.7 * np.random.standard_normal((D, N)) / np.sqrt(D) / s[:, None]
    A = np.random.standard_normal((N, R)) / np.sqrt(N) / t[:, None]
    Z_scale = (np.abs(Z).max(axis=1, keepdims=True) / 448).astype(np.float32)
    A_scale = (np.abs(A).max(axis=1, keepdims=True) / 448).astype(np.float32)
    return {"x": bf(x),
            "Z_bytes": e4m3fn_bytes(Z / f64(Z_scale)),
            "Z_scale": Z_scale,
            "A_bytes": e4m3fn_bytes(A / f64(A_scale)),
            "A_scale": A_scale,
            "az": bf(np.exp(0.3 * np.random.standard_normal(N)) * t),
            "ax": bf(np.exp(0.3 * np.random.standard_normal(M))),
            "offset": bf(0.5 * np.random.standard_normal(R))}


def reference(x, Z_bytes, Z_scale, A_bytes, A_scale, az, ax, offset):
    Z = e4m3fn_values(Z_bytes) * np.repeat(f64(Z_scale), N, axis=1)
    A = e4m3fn_values(A_bytes) * np.repeat(f64(A_scale), R, axis=1)
    S = mxq(f64(x), 1, "e4m3") @ mxq(Z, 0, "e4m3")
    E = np.exp(S) * f64(az)
    P = mxq(E, 1, "e4m3") @ mxq(A, 0, "e4m3")
    return P * f64(ax)[:, None] + f64(offset)

@@ -1,0 +1,408 @@
+from contextlib import ExitStack
+
+import concourse.mybir as mybir
+from concourse.masks import make_identity
+
+M, D, N, R = 1024, 1024, 2048, 1024
+FLOPS = 2 * M * D * N + 2 * M * N * R
+
+F32 = mybir.dt.float32
+BF16 = mybir.dt.bfloat16
+U32 = mybir.dt.uint32
+U8 = mybir.dt.uint8
+FP8 = mybir.dt.float8_e4m3fn
+FP8X4 = mybir.dt.float8_e4m3fn_x4
+ACT = mybir.ActivationFunctionType
+ALU = mybir.AluOpType
+
+P = 128
+W = 512
+KG = D // W
+NG = N // W
+RH = R // W
+QB = M // P
+CHUNKS = ((0, 4), (4, 2), (6, 2))
+LN_EDGE = 2.0 ** 62
+LN_TOP = 2.0 ** 64
+
+
+def tile_gp_mean_fp8_d5_kernel(tc, x, Z_bytes, Z_scale, A_bytes, A_scale, az, ax, offset, out):
+    nc = tc.nc
+    with ExitStack() as ctx:
+        const = ctx.enter_context(tc.tile_pool(name="const", bufs=1))
+        raw = ctx.enter_context(tc.tile_pool(name="raw", bufs=1))
+        work = ctx.enter_context(tc.tile_pool(name="work", bufs=8))
+        keep = ctx.enter_context(tc.tile_pool(name="keep", bufs=1))
+        res = ctx.enter_context(tc.tile_pool(name="res", bufs=6))
+        psum_s = ctx.enter_context(tc.psum_pool(name="psum_s", bufs=4))
+        psum_o = ctx.enter_context(tc.psum_pool(name="psum_o", bufs=4))
+
+        az_in = const.tile([P, NG, 4], BF16, name="az_in")
+        nc.scalar.dma_start(out=az_in[:], in_=az.rearrange("(g p t) -> p g t", p=P, t=4))
+        zs = const.tile([P, KG, 4], F32, name="zs")
+        nc.sync.dma_start(out=zs[:], in_=Z_scale.rearrange("(g p t) o -> p g (t o)", p=P, t=4))
+        zb = {}
+        z_src = Z_bytes.rearrange("(g p t) n -> g p t n", p=P, t=4)
+
+        def load_z(kg, g):
+            zb[kg, g] = raw.tile([P, 4, W], U8, name=f"z_bytes_{kg}_{g}")
+            nc.sync.dma_start(out=zb[kg, g][:], in_=z_src[kg][:, :, g * W:(g + 1) * W])
+
+        x_src = x.rearrange("(p b) d -> p b d", b=QB)
+        xs = {}
+
+        def load_x(h):
+            xs[h] = raw.tile([P, 4, D], BF16, name=f"x_rows_{h}")
+            nc.sync.dma_start(out=xs[h][:], in_=x_src[:, 4 * h:4 * h + 4, :])
+
+        ab = {}
+        a_src = A_bytes.rearrange("(g p t) n -> g p (t n)", p=P, t=4)
+
+        def load_a(g):
+            ab[g] = raw.tile([P, 4, R], U8, name=f"a_bytes_{g}")
+            nc.sync.dma_start(out=ab[g][:].rearrange("p t n -> p (t n)"), in_=a_src[g])
+
+        load_z(0, 0)
+        load_z(1, 0)
+        load_x(0)
+        for g in range(1, NG):
+            load_z(0, g)
+            load_z(1, g)
+        as_in = const.tile([P, NG, 4], F32, name="as_in")
+        nc.sync.dma_start(out=as_in[:], in_=A_scale.rearrange("(g p t) o -> p g (t o)", p=P, t=4))
+        load_x(1)
+        for g in range(NG):
+            load_a(g)
+        ax_in = const.tile([P, QB], BF16, name="ax_in")
+        nc.sync.dma_start(out=ax_in[:], in_=ax.rearrange("(p b) -> p b", b=QB))
+        off = const.tile([P, R], BF16, name="off")
+        nc.sync.dma_start(out=off[:], in_=offset.partition_broadcast(P))
+
+        ident = const.tile([P, P], F32, name="ident")
+        make_identity(nc, ident[:])
+
+        az_abs = const.tile([P, NG * 4], F32, name="az_abs")
+        az_sign = const.tile([P, NG * 4], F32, name="az_sign")
+        az_flat = az_in[:].rearrange("p g t -> p (g t)")
+        nc.scalar.activation(out=az_abs[:], in_=az_flat, func=ACT.Abs)
+        nc.scalar.activation(out=az_sign[:], in_=az_flat, func=ACT.Sign)
+        parts = const.tile([P, 3, NG * 4], F32, name="parts")
+        nc.gpsimd.tensor_scalar(out=parts[:, 0, :], in0=az_abs[:], scalar1=1.0 / LN_EDGE, scalar2=LN_TOP, op0=ALU.max, op1=ALU.min)
+        nc.gpsimd.tensor_scalar(out=parts[:, 1, :], in0=az_abs[:], scalar1=1.0 / LN_TOP, scalar2=1.0, op0=ALU.mult, op1=ALU.max)
+        low = const.tile([P, NG * 4], F32, name="low")
+        nc.gpsimd.tensor_scalar(out=low[:], in0=az_abs[:], scalar1=LN_EDGE, scalar2=1.0, op0=ALU.mult, op1=ALU.min)
+        nc.gpsimd.tensor_scalar(out=parts[:, 2, :], in0=low[:], scalar1=1.0 / LN_TOP, scalar2=1.0, op0=ALU.max, op1=ALU.mult)
+        logs = const.tile([P, 3, NG * 4], F32, name="logs")
+
+        def finish_logs():
+            nc.scalar.activation(out=logs[:], in_=parts[:], func=ACT.Ln)
+            nc.gpsimd.tensor_tensor(out=ln_sum1[:], in0=logs[:, 0, :], in1=logs[:, 1, :], op=ALU.add)
+            nc.gpsimd.tensor_tensor(out=ln_az[:], in0=ln_sum1[:], in1=logs[:, 2, :], op=ALU.add)
+
+        ln_sum1 = const.tile([P, NG * 4], F32, name="ln_sum1")
+        ln_az = const.tile([P, NG * 4], F32, name="ln_az")
+        a_scale = const.tile([P, NG * 4], F32, name="a_scale")
+
+        def widen(engine, dst, src, scale):
+            if engine == "S":
+                nc.scalar.activation(out=dst, in_=src.bitcast(FP8), func=ACT.Copy, scale=scale)
+            else:
+                nc.vector.tensor_scalar(out=dst, in0=src.bitcast(FP8), scalar1=scale, scalar2=None, op0=ALU.mult)
+
+        def copy(engine, dst, src):
+            if engine == "S":
+                nc.scalar.copy(out=dst, in_=src)
+            else:
+                nc.vector.tensor_copy(out=dst, in_=src)
+
+        planes = {}
+        mixed = {}
+        quant = {}
+
+        def zw(kg, g, who):
+            key = ("z", kg, g)
+            if key not in planes:
+                planes[key] = work.tile([P, 4, W], BF16, tag="planes", bufs=8, name=f"zw_{kg}_{g}")
+            for t in range(4):
+                if who[t] != ".":
+                    widen(who[t], planes[key][:, t, :], zb[kg, g][:, t, :], zs[:, kg, t:t + 1])
+
+        def aw(g, r, who):
+            key = ("a", g, r)
+            if key not in planes:
+                planes[key] = work.tile([P, 4, W], BF16, tag="planes", bufs=8, name=f"aw_{g}_{r}")
+            for t in range(4):
+                if who[t] != ".":
+                    widen(who[t], planes[key][:, t, :], ab[g][:, t, r * W:(r + 1) * W], a_scale[:, 4 * g + t:4 * g + t + 1])
+
+        def mix_tile(key, width):
+            if key not in mixed:
+                mixed[key] = work.tile([P, width, 4], BF16, tag="mixed" if width == W else "mixed2", bufs=7 if width == W else 4, name="mix_" + "_".join(str(v) for v in key), align_bytes=64)
+            return mixed[key]
+
+        def zi(kg, g, who):
+            key = ("z", kg, g)
+            dst = mix_tile(key, W)
+            step = 4 // len(who)
+            for i, e in enumerate(who):
+                t0 = i * step
+                copy(e,
+                     dst[:, t0 * P:(t0 + step) * P, :].rearrange("p (t c i) j -> p t c j i", t=step, i=4),
+                     planes[key][:].rearrange("p j (c i t) -> p t c j i", i=4, t=4)[:, t0:t0 + step])
+
+        def mix(key, who, width=W):
+            dst = mix_tile(key, width)
+            step = width // len(who)
+            for i, e in enumerate(who):
+                copy(e,
+                     dst[:, i * step:(i + 1) * step, :].rearrange("p (c i) t -> p c t i", i=4),
+                     planes[key][:, :, i * step:(i + 1) * step].rearrange("p t (c i) -> p c t i", i=4))
+
+        def q(key, width=W):
+            name = "_".join(str(v) for v in key)
+            codes = keep.tile([P, width], U32, name=f"codes_{name}", align_bytes=64)
+            scales = keep.tile([P, width], U8, name=f"scales_{name}", align_bytes=64)
+            nc.vector.quantize_mx(out=codes[:].bitcast(FP8X4), scales=scales[:], in_=mixed[key][:].rearrange("p n t -> p (n t)"))
+            quant[key] = (codes, scales)
+
+        xt_banks = {}
+
+        def xt(h, kg):
+            words = xs[h][:].rearrange("p b d -> p (b d)").bitcast(F32).rearrange("p (b w) -> p b w", b=4)
+            for pair in range(2):
+                bank = psum_o.tile([P, 2, 2 * P], F32, tag="o", name=f"xt_{h}_{kg}_{pair}")
+                xt_banks[h, kg, pair] = bank
+                for bb in range(2):
+                    for u in range(2):
+                        nc.tensor.transpose(
+                            bank[:, u, bb * P:(bb + 1) * P],
+                            words[:, 2 * pair + bb, 256 * kg + u:256 * (kg + 1):2],
+                            ident[:],
+                        )
+
+        def xc(h, kg, who):
+            dst = mix_tile(("x", h, kg), W)
+            xw = dst[:].rearrange("p q e -> p (q e)").bitcast(F32).rearrange("p (q u) -> p q u", u=2)
+            for pair in range(2):
+                copy(who[pair], xw[:, 2 * pair * P:2 * (pair + 1) * P, :], xt_banks[h, kg, pair][:].rearrange("p u q -> p q u"))
+
+        sbank = {}
+
+        def s_mm(c, g):
+            b0, nb = CHUNKS[c]
+            nq = nb * P
+            h, q0 = b0 // 4, (b0 % 4) * P
+            for t in range(4):
+                s = psum_s.tile([P, nq], F32, tag="s", name=f"s_{c}_{g}_{t}")
+                sbank[c, g, t] = s
+                for kg in range(KG):
+                    zc, zp = quant["z", kg, g]
+                    xcod, xsc = quant["x", h, kg]
+                    nc.tensor.matmul_mx(
+                        out=s[:],
+                        lhsT=zc[:, t * P:(t + 1) * P].bitcast(FP8X4),
+                        lhsT_scale=zp[:, t * P:(t + 1) * P],
+                        rhs=xcod[:, q0:q0 + nq].bitcast(FP8X4),
+                        rhs_scale=xsc[:, q0:q0 + nq],
+                        start=(kg == 0),
+                        stop=(kg == KG - 1),
+                    )
+
+        def s_exp(c, g):
+            nq = CHUNKS[c][1] * P
+            planes["e", c, g] = work.tile([P, 4, nq], BF16, tag=f"ep{nq}", bufs=3, name=f"ep_{c}_{g}")
+            for t in range(4):
+                nc.scalar.activation(out=planes["e", c, g][:, t, :], in_=sbank[c, g, t][:], func=ACT.Exp, bias=ln_az[:, 4 * g + t:4 * g + t + 1])
+
+        def ei(c, g, who):
+            mix(("e", c, g), who, CHUNKS[c][1] * P)
+
+        def eq(c, g):
+            q(("e", c, g), CHUNKS[c][1] * P)
+
+        banks = {}
+
+        def p_mm(c, b, gs, rs=range(RH)):
+            e0 = (b - CHUNKS[c][0]) * P
+            for r in rs:
+                if (b, r) not in banks:
+                    banks[b, r] = psum_o.tile([P, W], F32, tag="o", name=f"o_{b}_{r}")
+                for g in gs:
+                    ec, es = quant["e", c, g]
+                    ac, asc = quant["a", g, r]
+                    nc.tensor.matmul_mx(
+                        out=banks[b, r][:],
+                        lhsT=ec[:, e0:e0 + P].bitcast(FP8X4),
+                        lhsT_scale=es[:, e0:e0 + P],
+                        rhs=ac[:].bitcast(FP8X4),
+                        rhs_scale=asc[:],
+                        start=(g == 0),
+                        stop=(g == NG - 1),
+                    )
+
+        rows = {}
+        dst_rows = out.rearrange("(p b) r -> p b r", b=QB)
+
+        def fin(b, rs=range(RH)):
+            for r in rs:
+                rows[b, r] = res.tile([P, W], F32, tag="row", name=f"row_{b}_{r}")
+                cols = slice(r * W, (r + 1) * W)
+                nc.vector.scalar_tensor_tensor(
+                    out=rows[b, r][:], in0=banks[b, r][:], scalar=ax_in[:, b:b + 1], in1=off[:, cols], op0=ALU.mult, op1=ALU.add
+                )
+                nc.sync.dma_start(out=dst_rows[:, b, cols], in_=rows[b, r][:])
+
+        zw(0, 0, "VVVV")
+        zw(1, 0, "SSVV")
+        finish_logs()
+        zi(0, 0, "V")
+        xt(0, 0)
+        xt(0, 1)
+        xc(0, 0, "SS")
+        zi(1, 0, "V")
+        q(("z", 0, 0))
+        xc(0, 1, "SS")
+        zw(0, 1, "VVSS")
+        q(("z", 1, 0))
+        q(("x", 0, 0))
+        zw(1, 1, "SSSS")
+        q(("x", 0, 1))
+        s_mm(0, 0)
+        s_exp(0, 0)
+        zi(0, 1, "V")
+        zi(1, 1, "V")
+        q(("z", 0, 1))
+        zw(0, 2, "VVSS")
+        ei(0, 0, "V")
+        q(("z", 1, 1))
+        s_mm(0, 1)
+        eq(0, 0)
+        s_exp(0, 1)
+        zw(1, 2, "VSSS")
+        xt(1, 0)
+        xc(1, 0, "SS")
+        zi(0, 2, "V")
+        zi(1, 2, "V")
+        q(("z", 0, 2))
+        q(("x", 1, 0))
+        zw(0, 3, "VVSS")
+        ei(0, 1, "V")
+        q(("z", 1, 2))
+        eq(0, 1)
+        s_mm(0, 2)
+        s_exp(0, 2)
+        zw(1, 3, "VSSS")
+        xt(1, 1)
+        xc(1, 1, "SS")
+        zi(0, 3, "V")
+        zi(1, 3, "V")
+        q(("z", 0, 3))
+        q(("x", 1, 1))
+        nc.gpsimd.tensor_tensor(out=a_scale[:], in0=as_in[:].rearrange("p g t -> p (g t)"), in1=az_sign[:], op=ALU.mult)
+        ei(0, 2, "V")
+        q(("z", 1, 3))
+        eq(0, 2)
+        s_mm(0, 3)
+        s_exp(0, 3)
+        aw(0, 0, "SSSS")
+        s_mm(1, 0)
+        aw(1, 0, "SSSS")
+        s_exp(1, 0)
+        ei(0, 3, "V")
+        mix(("a", 0, 0), "V")
+        eq(0, 3)
+        q(("a", 0, 0))
+        s_mm(1, 1)
+        aw(2, 0, "SSSS")
+        s_exp(1, 1)
+        ei(1, 0, "V")
+        mix(("a", 1, 0), "V")
+        eq(1, 0)
+        q(("a", 1, 0))
+        p_mm(0, 0, [0, 1], [0])
+        p_mm(0, 1, [0, 1], [0])
+        p_mm(0, 2, [0, 1], [0])
+        p_mm(0, 3, [0, 1], [0])
+        aw(3, 0, "SSSS")
+        ei(1, 1, "V")
+        mix(("a", 2, 0), "V")
+        eq(1, 1)
+        q(("a", 2, 0))
+        p_mm(0, 0, [2], [0])
+        p_mm(0, 1, [2], [0])
+        p_mm(0, 2, [2], [0])
+        p_mm(0, 3, [2], [0])
+        s_mm(1, 2)
+        s_exp(1, 2)
+        aw(0, 1, "SSSS")
+        mix(("a", 3, 0), "V")
+        ei(1, 2, "S")
+        q(("a", 3, 0))
+        eq(1, 2)
+        p_mm(0, 0, [3], [0])
+        p_mm(0, 1, [3], [0])
+        p_mm(0, 2, [3], [0])
+        p_mm(0, 3, [3], [0])
+        s_mm(1, 3)
+        s_exp(1, 3)
+        aw(1, 1, "SSSS")
+        fin(0, [0])
+        fin(1, [0])
+        mix(("a", 0, 1), "V")
+        fin(2, [0])
+        q(("a", 0, 1))
+        fin(3, [0])
+        ei(1, 3, "S")
+        s_mm(2, 0)
+        s_exp(2, 0)
+        aw(2, 1, "SSSS")
+        mix(("a", 1, 1), "V")
+        eq(1, 3)
+        q(("a", 1, 1))
+        p_mm(1, 4, range(4), [0])
+        p_mm(1, 5, range(4), [0])
+        s_mm(2, 1)
+        ei(2, 0, "S")
+        fin(4, [0])
+        eq(2, 0)
+        fin(5, [0])
+        p_mm(0, 0, [0, 1], [1])
+        p_mm(0, 1, [0, 1], [1])
+        p_mm(0, 2, [0, 1], [1])
+        p_mm(0, 3, [0, 1], [1])
+        aw(3, 1, "SSSS")
+        mix(("a", 2, 1), "V")
+        s_exp(2, 1)
+        s_mm(2, 2)
+        q(("a", 2, 1))
+        p_mm(0, 0, [2], [1])
+        p_mm(0, 1, [2], [1])
+        p_mm(0, 2, [2], [1])
+        p_mm(0, 3, [2], [1])
+        s_exp(2, 2)
+        s_mm(2, 3)
+        mix(("a", 3, 1), "V")
+        ei(2, 1, "S")
+        q(("a", 3, 1))
+        p_mm(0, 0, [3], [1])
+        p_mm(0, 1, [3], [1])
+        p_mm(0, 2, [3], [1])
+        p_mm(0, 3, [3], [1])
+        ei(2, 2, "S")
+        eq(2, 1)
+        s_exp(2, 3)
+        fin(0, [1])
+        fin(1, [1])
+        eq(2, 2)
+        p_mm(1, 4, range(4), [1])
+        p_mm(1, 5, range(4), [1])
+        fin(2, [1])
+        ei(2, 3, "V")
+        fin(3, [1])
+        eq(2, 3)
+        fin(4, [1])
+        fin(5, [1])
+        p_mm(2, 6, range(4))
+        p_mm(2, 7, range(4))
+        fin(6)
+        fin(7)

@@ -36,11 +36,12 @@ def tile_gp_mean_fp8_d5_kernel(tc, x, Z_bytes, Z_scale, A_bytes, A_scale, az, ax
         res = ctx.enter_context(tc.tile_pool(name="res", bufs=6))
         psum_s = ctx.enter_context(tc.psum_pool(name="psum_s", bufs=4))
         psum_o = ctx.enter_context(tc.psum_pool(name="psum_o", bufs=4))
+        ctx.enter_context(tc.manual_schedule())
 
         az_in = const.tile([P, NG, 4], BF16, name="az_in")
         nc.scalar.dma_start(out=az_in[:], in_=az.rearrange("(g p t) -> p g t", p=P, t=4))
         zs = const.tile([P, KG, 4], F32, name="zs")
-        nc.sync.dma_start(out=zs[:], in_=Z_scale.rearrange("(g p t) o -> p g (t o)", p=P, t=4))
+        nc.scalar.dma_start(out=zs[:], in_=Z_scale.rearrange("(g p t) o -> p g (t o)", p=P, t=4))
         zb = {}
         z_src = Z_bytes.rearrange("(g p t) n -> g p t n", p=P, t=4)
 
@@ -81,11 +82,13 @@ def tile_gp_mean_fp8_d5_kernel(tc, x, Z_bytes, Z_scale, A_bytes, A_scale, az, ax
         ident = const.tile([P, P], F32, name="ident")
         make_identity(nc, ident[:])
 
-        az_abs = const.tile([P, NG * 4], F32, name="az_abs")
-        az_sign = const.tile([P, NG * 4], F32, name="az_sign")
         az_flat = az_in[:].rearrange("p g t -> p (g t)")
-        nc.scalar.activation(out=az_abs[:], in_=az_flat, func=ACT.Abs)
-        nc.scalar.activation(out=az_sign[:], in_=az_flat, func=ACT.Sign)
+        az_step = const.tile([P, NG * 4], F32, name="az_step")
+        nc.gpsimd.tensor_scalar(out=az_step[:], in0=az_flat, scalar1=0.0, scalar2=2.0, op0=ALU.is_ge, op1=ALU.mult)
+        az_sign = const.tile([P, NG * 4], F32, name="az_sign")
+        nc.gpsimd.tensor_scalar(out=az_sign[:], in0=az_step[:], scalar1=-1.0, scalar2=1.0, op0=ALU.add, op1=ALU.mult)
+        az_abs = const.tile([P, NG * 4], F32, name="az_abs")
+        nc.gpsimd.tensor_tensor(out=az_abs[:], in0=az_flat, in1=az_sign[:], op=ALU.mult)
         parts = const.tile([P, 3, NG * 4], F32, name="parts")
         nc.gpsimd.tensor_scalar(out=parts[:, 0, :], in0=az_abs[:], scalar1=1.0 / LN_EDGE, scalar2=LN_TOP, op0=ALU.max, op1=ALU.min)
         nc.gpsimd.tensor_scalar(out=parts[:, 1, :], in0=az_abs[:], scalar1=1.0 / LN_TOP, scalar2=1.0, op0=ALU.mult, op1=ALU.max)
@@ -98,10 +101,12 @@ def tile_gp_mean_fp8_d5_kernel(tc, x, Z_bytes, Z_scale, A_bytes, A_scale, az, ax
             nc.scalar.activation(out=logs[:], in_=parts[:], func=ACT.Ln)
             nc.gpsimd.tensor_tensor(out=ln_sum1[:], in0=logs[:, 0, :], in1=logs[:, 1, :], op=ALU.add)
             nc.gpsimd.tensor_tensor(out=ln_az[:], in0=ln_sum1[:], in1=logs[:, 2, :], op=ALU.add)
+            nc.gpsimd.tensor_tensor(out=a_scale[:], in0=as_in[:].rearrange("p g t -> p (g t)"), in1=az_sign[:], op=ALU.mult)
+
+        a_scale = const.tile([P, NG * 4], F32, name="a_scale")
 
         ln_sum1 = const.tile([P, NG * 4], F32, name="ln_sum1")
         ln_az = const.tile([P, NG * 4], F32, name="ln_az")
-        a_scale = const.tile([P, NG * 4], F32, name="a_scale")
 
         def widen(engine, dst, src, scale):
             if engine == "S":
@@ -137,7 +142,7 @@ def tile_gp_mean_fp8_d5_kernel(tc, x, Z_bytes, Z_scale, A_bytes, A_scale, az, ax
 
         def mix_tile(key, width):
             if key not in mixed:
-                mixed[key] = work.tile([P, width, 4], BF16, tag="mixed" if width == W else "mixed2", bufs=7 if width == W else 4, name="mix_" + "_".join(str(v) for v in key), align_bytes=64)
+                mixed[key] = work.tile([P, width, 4], BF16, tag="mixed" if width == W else "mixed2", bufs=8 if width == W else 4, name="mix_" + "_".join(str(v) for v in key), align_bytes=64)
             return mixed[key]
 
         def zi(kg, g, who):
@@ -186,33 +191,29 @@ def tile_gp_mean_fp8_d5_kernel(tc, x, Z_bytes, Z_scale, A_bytes, A_scale, az, ax
             for pair in range(2):
                 copy(who[pair], xw[:, 2 * pair * P:2 * (pair + 1) * P, :], xt_banks[h, kg, pair][:].rearrange("p u q -> p q u"))
 
-        sbank = {}
-
-        def s_mm(c, g):
+        def stage1(c, g):
             b0, nb = CHUNKS[c]
             nq = nb * P
             h, q0 = b0 // 4, (b0 % 4) * P
-            for t in range(4):
-                s = psum_s.tile([P, nq], F32, tag="s", name=f"s_{c}_{g}_{t}")
-                sbank[c, g, t] = s
-                for kg in range(KG):
-                    zc, zp = quant["z", kg, g]
-                    xcod, xsc = quant["x", h, kg]
-                    nc.tensor.matmul_mx(
-                        out=s[:],
-                        lhsT=zc[:, t * P:(t + 1) * P].bitcast(FP8X4),
-                        lhsT_scale=zp[:, t * P:(t + 1) * P],
-                        rhs=xcod[:, q0:q0 + nq].bitcast(FP8X4),
-                        rhs_scale=xsc[:, q0:q0 + nq],
-                        start=(kg == 0),
-                        stop=(kg == KG - 1),
-                    )
-
-        def s_exp(c, g):
-            nq = CHUNKS[c][1] * P
             planes["e", c, g] = work.tile([P, 4, nq], BF16, tag=f"ep{nq}", bufs=3, name=f"ep_{c}_{g}")
-            for t in range(4):
-                nc.scalar.activation(out=planes["e", c, g][:, t, :], in_=sbank[c, g, t][:], func=ACT.Exp, bias=ln_az[:, 4 * g + t:4 * g + t + 1])
+            sums = {}
+            for t in range(5):
+                if t < 4:
+                    sums[t] = psum_s.tile([P, nq], F32, tag="s", name=f"s_{c}_{g}_{t}")
+                    for kg in range(KG):
+                        zc, zp = quant["z", kg, g]
+                        xcod, xsc = quant["x", h, kg]
+                        nc.tensor.matmul_mx(
+                            out=sums[t][:],
+                            lhsT=zc[:, t * P:(t + 1) * P].bitcast(FP8X4),
+                            lhsT_scale=zp[:, t * P:(t + 1) * P],
+                            rhs=xcod[:, q0:q0 + nq].bitcast(FP8X4),
+                            rhs_scale=xsc[:, q0:q0 + nq],
+                            start=(kg == 0),
+                            stop=(kg == KG - 1),
+                        )
+                if t > 0:
+                    nc.scalar.activation(out=planes["e", c, g][:, t - 1, :], in_=sums[t - 1][:], func=ACT.Exp, bias=ln_az[:, 4 * g + t - 1:4 * g + t])
 
         def ei(c, g, who):
             mix(("e", c, g), who, CHUNKS[c][1] * P)
@@ -252,157 +253,148 @@ def tile_gp_mean_fp8_d5_kernel(tc, x, Z_bytes, Z_scale, A_bytes, A_scale, az, ax
                 )
                 nc.sync.dma_start(out=dst_rows[:, b, cols], in_=rows[b, r][:])
 
-        zw(0, 0, "VVVV")
+        zw(0, 0, "SVSV")
         zw(1, 0, "SSVV")
-        finish_logs()
         zi(0, 0, "V")
-        xt(0, 0)
+        finish_logs()
         xt(0, 1)
-        xc(0, 0, "SS")
-        zi(1, 0, "V")
+        zi(1, 0, "SV")
         q(("z", 0, 0))
-        xc(0, 1, "SS")
-        zw(0, 1, "VVSS")
         q(("z", 1, 0))
-        q(("x", 0, 0))
-        zw(1, 1, "SSSS")
-        q(("x", 0, 1))
-        s_mm(0, 0)
-        s_exp(0, 0)
-        zi(0, 1, "V")
-        zi(1, 1, "V")
-        q(("z", 0, 1))
-        zw(0, 2, "VVSS")
-        ei(0, 0, "V")
-        q(("z", 1, 1))
-        s_mm(0, 1)
-        eq(0, 0)
-        s_exp(0, 1)
-        zw(1, 2, "VSSS")
+        zw(0, 1, "VVVV")
+        xc(0, 1, "SS")
+        xt(0, 0)
+        zw(1, 1, "VSVV")
+        zw(1, 2, "VSVS")
         xt(1, 0)
-        xc(1, 0, "SS")
-        zi(0, 2, "V")
-        zi(1, 2, "V")
-        q(("z", 0, 2))
-        q(("x", 1, 0))
-        zw(0, 3, "VVSS")
-        ei(0, 1, "V")
-        q(("z", 1, 2))
-        eq(0, 1)
-        s_mm(0, 2)
-        s_exp(0, 2)
-        zw(1, 3, "VSSS")
+        xc(0, 0, "SS")
+        zw(0, 3, "VSVV")
+        q(("x", 0, 1))
+        zi(0, 1, "V")
+        q(("x", 0, 0))
+        zi(1, 1, "VS")
+        zi(1, 2, "VS")
+        xc(1, 0, "SV")
+        stage1(0, 0)
         xt(1, 1)
         xc(1, 1, "SS")
+        zw(1, 3, "VVVV")
+        q(("z", 0, 1))
+        q(("z", 1, 1))
         zi(0, 3, "V")
+        q(("x", 1, 0))
         zi(1, 3, "V")
-        q(("z", 0, 3))
+        zw(0, 2, "VVSV")
         q(("x", 1, 1))
-        nc.gpsimd.tensor_tensor(out=a_scale[:], in0=as_in[:].rearrange("p g t -> p (g t)"), in1=az_sign[:], op=ALU.mult)
-        ei(0, 2, "V")
+        stage1(0, 1)
+        q(("z", 1, 2))
+        stage1(1, 1)
+        zi(0, 2, "V")
+        aw(0, 0, "VSSS")
+        q(("z", 0, 2))
+        ei(0, 0, "V")
+        stage1(1, 2)
+        q(("z", 0, 3))
         q(("z", 1, 3))
-        eq(0, 2)
-        s_mm(0, 3)
-        s_exp(0, 3)
-        aw(0, 0, "SSSS")
-        s_mm(1, 0)
-        aw(1, 0, "SSSS")
-        s_exp(1, 0)
-        ei(0, 3, "V")
-        mix(("a", 0, 0), "V")
-        eq(0, 3)
-        q(("a", 0, 0))
-        s_mm(1, 1)
-        aw(2, 0, "SSSS")
-        s_exp(1, 1)
-        ei(1, 0, "V")
-        mix(("a", 1, 0), "V")
-        eq(1, 0)
-        q(("a", 1, 0))
-        p_mm(0, 0, [0, 1], [0])
-        p_mm(0, 1, [0, 1], [0])
-        p_mm(0, 2, [0, 1], [0])
-        p_mm(0, 3, [0, 1], [0])
-        aw(3, 0, "SSSS")
+        stage1(1, 0)
+        stage1(0, 3)
+        ei(0, 1, "V")
+        ei(1, 2, "V")
+        eq(0, 1)
+        stage1(0, 2)
+        aw(2, 0, "VVSV")
+        aw(1, 0, "VSVS")
         ei(1, 1, "V")
+        mix(("a", 0, 0), "V")
+        ei(0, 3, "V")
+        aw(3, 0, "VVVV")
         mix(("a", 2, 0), "V")
-        eq(1, 1)
+        stage1(1, 3)
+        mix(("a", 1, 0), "SV")
+        eq(1, 2)
+        eq(0, 0)
+        q(("a", 0, 0))
+        q(("a", 1, 0))
+        stage1(2, 0)
+        ei(1, 0, "VS")
         q(("a", 2, 0))
+        ei(0, 2, "SV")
+        mix(("a", 3, 0), "VS")
+        stage1(2, 1)
+        eq(0, 2)
+        aw(3, 1, "SSSS")
+        p_mm(0, 2, [0, 1], [0])
+        eq(0, 3)
+        p_mm(0, 1, [0, 1], [0])
+        q(("a", 3, 0))
+        p_mm(0, 0, [0, 1], [0])
+        p_mm(0, 3, [0, 1], [0])
         p_mm(0, 0, [2], [0])
+        eq(1, 0)
+        p_mm(0, 3, [2], [0])
         p_mm(0, 1, [2], [0])
         p_mm(0, 2, [2], [0])
-        p_mm(0, 3, [2], [0])
-        s_mm(1, 2)
-        s_exp(1, 2)
-        aw(0, 1, "SSSS")
-        mix(("a", 3, 0), "V")
-        ei(1, 2, "S")
-        q(("a", 3, 0))
-        eq(1, 2)
-        p_mm(0, 0, [3], [0])
-        p_mm(0, 1, [3], [0])
         p_mm(0, 2, [3], [0])
+        eq(1, 1)
         p_mm(0, 3, [3], [0])
-        s_mm(1, 3)
-        s_exp(1, 3)
-        aw(1, 1, "SSSS")
-        fin(0, [0])
-        fin(1, [0])
-        mix(("a", 0, 1), "V")
+        aw(0, 1, "VVSV")
         fin(2, [0])
-        q(("a", 0, 1))
-        fin(3, [0])
-        ei(1, 3, "S")
-        s_mm(2, 0)
-        s_exp(2, 0)
-        aw(2, 1, "SSSS")
-        mix(("a", 1, 1), "V")
+        ei(1, 3, "V")
+        p_mm(0, 1, [3], [0])
+        fin(1, [0])
         eq(1, 3)
-        q(("a", 1, 1))
-        p_mm(1, 4, range(4), [0])
-        p_mm(1, 5, range(4), [0])
-        s_mm(2, 1)
+        mix(("a", 0, 1), "V")
+        aw(1, 1, "VSSV")
+        p_mm(0, 0, [3], [0])
+        aw(2, 1, "VSSS")
+        mix(("a", 1, 1), "SV")
+        fin(0, [0])
+        stage1(2, 2)
+        p_mm(1, 5, [0, 1, 2, 3], [0])
+        mix(("a", 3, 1), "S")
         ei(2, 0, "S")
-        fin(4, [0])
-        eq(2, 0)
-        fin(5, [0])
-        p_mm(0, 0, [0, 1], [1])
-        p_mm(0, 1, [0, 1], [1])
-        p_mm(0, 2, [0, 1], [1])
-        p_mm(0, 3, [0, 1], [1])
-        aw(3, 1, "SSSS")
+        fin(3, [0])
+        q(("a", 0, 1))
+        p_mm(1, 4, [0, 1, 2, 3], [0])
+        stage1(2, 3)
+        q(("a", 1, 1))
         mix(("a", 2, 1), "V")
-        s_exp(2, 1)
-        s_mm(2, 2)
+        fin(5, [0])
+        p_mm(0, 1, [0, 1], [1])
         q(("a", 2, 1))
-        p_mm(0, 0, [2], [1])
-        p_mm(0, 1, [2], [1])
-        p_mm(0, 2, [2], [1])
-        p_mm(0, 3, [2], [1])
-        s_exp(2, 2)
-        s_mm(2, 3)
-        mix(("a", 3, 1), "V")
-        ei(2, 1, "S")
+        fin(4, [0])
+        p_mm(0, 2, [0, 1], [1])
         q(("a", 3, 1))
-        p_mm(0, 0, [3], [1])
+        p_mm(0, 3, [0, 1], [1])
+        ei(2, 1, "S")
+        ei(2, 2, "V")
+        p_mm(0, 2, [2], [1])
+        ei(2, 3, "S")
+        p_mm(0, 1, [2], [1])
+        p_mm(1, 5, [0, 1, 2, 3], [1])
+        eq(2, 0)
         p_mm(0, 1, [3], [1])
         p_mm(0, 2, [3], [1])
-        p_mm(0, 3, [3], [1])
-        ei(2, 2, "S")
-        eq(2, 1)
-        s_exp(2, 3)
-        fin(0, [1])
         fin(1, [1])
-        eq(2, 2)
-        p_mm(1, 4, range(4), [1])
-        p_mm(1, 5, range(4), [1])
         fin(2, [1])
-        ei(2, 3, "V")
+        p_mm(0, 3, [2], [1])
+        p_mm(0, 3, [3], [1])
+        eq(2, 2)
         fin(3, [1])
-        eq(2, 3)
-        fin(4, [1])
+        p_mm(0, 0, [0, 1], [1])
+        p_mm(0, 0, [2], [1])
+        p_mm(0, 0, [3], [1])
+        eq(2, 1)
+        p_mm(1, 4, [0, 1, 2, 3], [1])
         fin(5, [1])
-        p_mm(2, 6, range(4))
-        p_mm(2, 7, range(4))
-        fin(6)
-        fin(7)
+        eq(2, 3)
+        p_mm(2, 7, [0, 1, 2, 3], [1])
+        fin(4, [1])
+        fin(0, [1])
+        p_mm(2, 6, [0, 1, 2, 3], [0])
+        fin(7, [1])
+        fin(6, [0])
+        p_mm(2, 7, [0, 1, 2, 3], [0])
+        fin(7, [0])
+        p_mm(2, 6, [0, 1, 2, 3], [1])
+        fin(6, [1])

@@ -17,13 +17,15 @@ ALU = mybir.AluOpType
 
 P = 128
 W = 512
+UNIT = 2 * W
 KG = D // W
 NG = N // W
-RH = R // W
 QB = M // P
+CB = W // P
 CHUNKS = ((0, 4), (4, 2), (6, 2))
 LN_EDGE = 2.0 ** 62
 LN_TOP = 2.0 ** 64
+LN_MIN = 2.0 ** -126
 
 
 def tile_gp_mean_fp8_d5_kernel(tc, x, Z_bytes, Z_scale, A_bytes, A_scale, az, ax, offset, out):
@@ -31,49 +33,44 @@ def tile_gp_mean_fp8_d5_kernel(tc, x, Z_bytes, Z_scale, A_bytes, A_scale, az, ax
     with ExitStack() as ctx:
         const = ctx.enter_context(tc.tile_pool(name="const", bufs=1))
         raw = ctx.enter_context(tc.tile_pool(name="raw", bufs=1))
-        work = ctx.enter_context(tc.tile_pool(name="work", bufs=8))
+        work = ctx.enter_context(tc.tile_pool(name="work", bufs=6))
         keep = ctx.enter_context(tc.tile_pool(name="keep", bufs=1))
         res = ctx.enter_context(tc.tile_pool(name="res", bufs=6))
-        psum_s = ctx.enter_context(tc.psum_pool(name="psum_s", bufs=4))
-        psum_o = ctx.enter_context(tc.psum_pool(name="psum_o", bufs=4))
+        psum = ctx.enter_context(tc.psum_pool(name="psum", bufs=1))
         ctx.enter_context(tc.manual_schedule())
 
         az_in = const.tile([P, NG, 4], BF16, name="az_in")
         nc.scalar.dma_start(out=az_in[:], in_=az.rearrange("(g p t) -> p g t", p=P, t=4))
         zs = const.tile([P, KG, 4], F32, name="zs")
         nc.scalar.dma_start(out=zs[:], in_=Z_scale.rearrange("(g p t) o -> p g (t o)", p=P, t=4))
-        zb = {}
-        z_src = Z_bytes.rearrange("(g p t) n -> g p t n", p=P, t=4)
 
-        def load_z(kg, g):
-            zb[kg, g] = raw.tile([P, 4, W], U8, name=f"z_bytes_{kg}_{g}")
-            nc.sync.dma_start(out=zb[kg, g][:], in_=z_src[kg][:, :, g * W:(g + 1) * W])
+        z_src = Z_bytes.rearrange("(g p t) n -> g p t n", p=P, t=4)
+        z_bytes = {(kg, h): raw.tile([P, 4, UNIT], U8, name=f"z_bytes_{kg}_{h}") for kg in range(KG) for h in range(2)}
+
+        def load_z(kg, h, lo, hi):
+            nc.sync.dma_start(out=z_bytes[kg, h][:, :, lo:hi], in_=z_src[kg][:, :, h * UNIT + lo:h * UNIT + hi])
 
         x_src = x.rearrange("(p b) d -> p b d", b=QB)
-        xs = {}
+        x_rows = {h: raw.tile([P, CB, D], BF16, name=f"x_rows_{h}") for h in range(2)}
 
         def load_x(h):
-            xs[h] = raw.tile([P, 4, D], BF16, name=f"x_rows_{h}")
-            nc.sync.dma_start(out=xs[h][:], in_=x_src[:, 4 * h:4 * h + 4, :])
+            nc.sync.dma_start(out=x_rows[h][:], in_=x_src[:, CB * h:CB * (h + 1), :])
 
-        ab = {}
-        a_src = A_bytes.rearrange("(g p t) n -> g p (t n)", p=P, t=4)
-
-        def load_a(g):
-            ab[g] = raw.tile([P, 4, R], U8, name=f"a_bytes_{g}")
-            nc.sync.dma_start(out=ab[g][:].rearrange("p t n -> p (t n)"), in_=a_src[g])
-
-        load_z(0, 0)
-        load_z(1, 0)
+        load_z(0, 0, 0, W)
+        load_z(1, 0, 0, W)
+        load_z(0, 0, W, UNIT)
+        load_z(1, 0, W, UNIT)
         load_x(0)
-        for g in range(1, NG):
-            load_z(0, g)
-            load_z(1, g)
+        load_z(0, 1, 0, UNIT)
+        load_z(1, 1, 0, UNIT)
         as_in = const.tile([P, NG, 4], F32, name="as_in")
         nc.sync.dma_start(out=as_in[:], in_=A_scale.rearrange("(g p t) o -> p g (t o)", p=P, t=4))
         load_x(1)
+        a_src = A_bytes.rearrange("(g p t) n -> g p (t n)", p=P, t=4)
+        a_bytes = {}
         for g in range(NG):
-            load_a(g)
+            a_bytes[g] = raw.tile([P, 4, R], U8, name=f"a_bytes_{g}")
+            nc.sync.dma_start(out=a_bytes[g][:].rearrange("p t n -> p (t n)"), in_=a_src[g])
         ax_in = const.tile([P, QB], BF16, name="ax_in")
         nc.sync.dma_start(out=ax_in[:], in_=ax.rearrange("(p b) -> p b", b=QB))
         off = const.tile([P, R], BF16, name="off")
@@ -83,30 +80,31 @@ def tile_gp_mean_fp8_d5_kernel(tc, x, Z_bytes, Z_scale, A_bytes, A_scale, az, ax
         make_identity(nc, ident[:])
 
         az_flat = az_in[:].rearrange("p g t -> p (g t)")
+        az_abs = const.tile([P, NG * 4], F32, name="az_abs")
+        nc.vector.scalar_tensor_tensor(out=az_abs[:], in0=az_flat, scalar=-1.0, in1=az_flat, op0=ALU.mult, op1=ALU.max)
+        low = const.tile([P, NG * 4], F32, name="low")
+        nc.vector.tensor_scalar(out=low[:], in0=az_abs[:], scalar1=LN_MIN, scalar2=LN_EDGE, op0=ALU.max, op1=ALU.mult)
+        parts = const.tile([P, 3, NG * 4], F32, name="parts")
+        nc.vector.tensor_scalar(out=parts[:, 0, :], in0=az_abs[:], scalar1=1.0 / LN_EDGE, scalar2=LN_TOP, op0=ALU.max, op1=ALU.min)
+        nc.vector.tensor_scalar(out=parts[:, 1, :], in0=az_abs[:], scalar1=1.0 / LN_TOP, scalar2=1.0, op0=ALU.mult, op1=ALU.max)
+        nc.vector.tensor_scalar(out=parts[:, 2, :], in0=low[:], scalar1=1.0, scalar2=1.0, op0=ALU.min, op1=ALU.mult)
         az_step = const.tile([P, NG * 4], F32, name="az_step")
         nc.gpsimd.tensor_scalar(out=az_step[:], in0=az_flat, scalar1=0.0, scalar2=2.0, op0=ALU.is_ge, op1=ALU.mult)
         az_sign = const.tile([P, NG * 4], F32, name="az_sign")
         nc.gpsimd.tensor_scalar(out=az_sign[:], in0=az_step[:], scalar1=-1.0, scalar2=1.0, op0=ALU.add, op1=ALU.mult)
-        az_abs = const.tile([P, NG * 4], F32, name="az_abs")
-        nc.gpsimd.tensor_tensor(out=az_abs[:], in0=az_flat, in1=az_sign[:], op=ALU.mult)
-        parts = const.tile([P, 3, NG * 4], F32, name="parts")
-        nc.gpsimd.tensor_scalar(out=parts[:, 0, :], in0=az_abs[:], scalar1=1.0 / LN_EDGE, scalar2=LN_TOP, op0=ALU.max, op1=ALU.min)
-        nc.gpsimd.tensor_scalar(out=parts[:, 1, :], in0=az_abs[:], scalar1=1.0 / LN_TOP, scalar2=1.0, op0=ALU.mult, op1=ALU.max)
-        low = const.tile([P, NG * 4], F32, name="low")
-        nc.gpsimd.tensor_scalar(out=low[:], in0=az_abs[:], scalar1=LN_EDGE, scalar2=1.0, op0=ALU.mult, op1=ALU.min)
-        nc.gpsimd.tensor_scalar(out=parts[:, 2, :], in0=low[:], scalar1=1.0 / LN_TOP, scalar2=1.0, op0=ALU.max, op1=ALU.mult)
         logs = const.tile([P, 3, NG * 4], F32, name="logs")
-
-        def finish_logs():
-            nc.scalar.activation(out=logs[:], in_=parts[:], func=ACT.Ln)
-            nc.gpsimd.tensor_tensor(out=ln_sum1[:], in0=logs[:, 0, :], in1=logs[:, 1, :], op=ALU.add)
-            nc.gpsimd.tensor_tensor(out=ln_az[:], in0=ln_sum1[:], in1=logs[:, 2, :], op=ALU.add)
-            nc.gpsimd.tensor_tensor(out=a_scale[:], in0=as_in[:].rearrange("p g t -> p (g t)"), in1=az_sign[:], op=ALU.mult)
-
+        ln_two = const.tile([P, NG * 4], F32, name="ln_two")
+        ln_az = const.tile([P, NG * 4], F32, name="ln_az")
         a_scale = const.tile([P, NG * 4], F32, name="a_scale")
 
-        ln_sum1 = const.tile([P, NG * 4], F32, name="ln_sum1")
-        ln_az = const.tile([P, NG * 4], F32, name="ln_az")
+        ax_f32 = const.tile([P, QB], F32, name="ax_f32")
+
+        def take_logs():
+            nc.scalar.activation(out=logs[:], in_=parts[:], func=ACT.Ln)
+            nc.gpsimd.tensor_tensor(out=ln_two[:], in0=logs[:, 0, :], in1=logs[:, 1, :], op=ALU.add)
+            nc.gpsimd.tensor_tensor(out=ln_az[:], in0=ln_two[:], in1=logs[:, 2, :], op=ALU.add)
+            nc.gpsimd.tensor_tensor(out=a_scale[:], in0=as_in[:].rearrange("p g t -> p (g t)"), in1=az_sign[:], op=ALU.mult)
+            nc.gpsimd.tensor_copy(out=ax_f32[:], in_=ax_in[:])
 
         def widen(engine, dst, src, scale):
             if engine == "S":
@@ -122,279 +120,287 @@ def tile_gp_mean_fp8_d5_kernel(tc, x, Z_bytes, Z_scale, A_bytes, A_scale, az, ax
 
         planes = {}
         mixed = {}
-        quant = {}
+        codes = {}
+        scales = {}
 
-        def zw(kg, g, who):
-            key = ("z", kg, g)
-            if key not in planes:
-                planes[key] = work.tile([P, 4, W], BF16, tag="planes", bufs=8, name=f"zw_{kg}_{g}")
-            for t in range(4):
-                if who[t] != ".":
-                    widen(who[t], planes[key][:, t, :], zb[kg, g][:, t, :], zs[:, kg, t:t + 1])
+        def plane_tile(unit):
+            if unit not in planes:
+                planes[unit] = work.tile([P, 4, UNIT], BF16, tag="planes", name="planes_" + "_".join(str(v) for v in unit))
+            return planes[unit]
 
-        def aw(g, r, who):
-            key = ("a", g, r)
-            if key not in planes:
-                planes[key] = work.tile([P, 4, W], BF16, tag="planes", bufs=8, name=f"aw_{g}_{r}")
-            for t in range(4):
-                if who[t] != ".":
-                    widen(who[t], planes[key][:, t, :], ab[g][:, t, r * W:(r + 1) * W], a_scale[:, 4 * g + t:4 * g + t + 1])
+        def mixed_tile(unit):
+            if unit not in mixed:
+                mixed[unit] = work.tile([P, UNIT, 4], BF16, tag="mixed", name="mixed_" + "_".join(str(v) for v in unit), align_bytes=64)
+            return mixed[unit]
 
-        def mix_tile(key, width):
-            if key not in mixed:
-                mixed[key] = work.tile([P, width, 4], BF16, tag="mixed" if width == W else "mixed2", bufs=8 if width == W else 4, name="mix_" + "_".join(str(v) for v in key), align_bytes=64)
-            return mixed[key]
+        def widen_z(kg, h, who):
+            dst = plane_tile(("z", kg, h))
+            step = 4 * UNIT // len(who)
+            for i, engine in enumerate(who):
+                t, lo = i % 4, i // 4 * step
+                widen(engine, dst[:, t, lo:lo + step], z_bytes[kg, h][:, t, lo:lo + step], zs[:, kg, t:t + 1])
 
-        def zi(kg, g, who):
-            key = ("z", kg, g)
-            dst = mix_tile(key, W)
-            step = 4 // len(who)
-            for i, e in enumerate(who):
-                t0 = i * step
-                copy(e,
-                     dst[:, t0 * P:(t0 + step) * P, :].rearrange("p (t c i) j -> p t c j i", t=step, i=4),
-                     planes[key][:].rearrange("p j (c i t) -> p t c j i", i=4, t=4)[:, t0:t0 + step])
+        def widen_a(pair, r, who):
+            dst = plane_tile(("a", pair, r))
+            for i, engine in enumerate(who):
+                t, half = i % 4, i // 4
+                g = 2 * pair + half
+                widen(engine, dst[:, t, half * W:(half + 1) * W], a_bytes[g][:, t, r * W:(r + 1) * W], a_scale[:, 4 * g + t:4 * g + t + 1])
 
-        def mix(key, who, width=W):
-            dst = mix_tile(key, width)
-            step = width // len(who)
-            for i, e in enumerate(who):
-                copy(e,
-                     dst[:, i * step:(i + 1) * step, :].rearrange("p (c i) t -> p c t i", i=4),
-                     planes[key][:, :, i * step:(i + 1) * step].rearrange("p t (c i) -> p c t i", i=4))
+        def mix(unit, who):
+            dst, src = mixed_tile(unit), planes[unit]
+            step = UNIT // len(who)
+            for i, engine in enumerate(who):
+                lo = i * step
+                if unit[0] == "z":
+                    half, t0, tiles = lo // W, lo % W // P, step // P
+                    copy(engine,
+                         dst[:, lo:lo + step, :].rearrange("p (t c i) j -> p t c j i", t=tiles, i=4),
+                         src[:, :, half * W:(half + 1) * W].rearrange("p j (c i t) -> p t c j i", i=4, t=4)[:, t0:t0 + tiles])
+                else:
+                    copy(engine,
+                         dst[:, lo:lo + step, :].rearrange("p (c i) t -> p c t i", i=4),
+                         src[:, :, lo:lo + step].rearrange("p t (c i) -> p c t i", i=4))
 
-        def q(key, width=W):
-            name = "_".join(str(v) for v in key)
-            codes = keep.tile([P, width], U32, name=f"codes_{name}", align_bytes=64)
-            scales = keep.tile([P, width], U8, name=f"scales_{name}", align_bytes=64)
-            nc.vector.quantize_mx(out=codes[:].bitcast(FP8X4), scales=scales[:], in_=mixed[key][:].rearrange("p n t -> p (n t)"))
-            quant[key] = (codes, scales)
+        def quantize(unit, part, parts_in_all):
+            name = "_".join(str(v) for v in unit)
+            if unit not in codes:
+                codes[unit] = keep.tile([P, UNIT], U32, name=f"codes_{name}", align_bytes=64)
+                scales[unit] = keep.tile([P, UNIT], U8, name=f"scales_{name}", align_bytes=64)
+            step = UNIT // parts_in_all
+            cols = slice(part * step, (part + 1) * step)
+            nc.vector.quantize_mx(
+                out=codes[unit][:, cols].bitcast(FP8X4), scales=scales[unit][:, cols], in_=mixed[unit][:, cols, :].rearrange("p n t -> p (n t)")
+            )
 
-        xt_banks = {}
+        free_banks = list(range(8))
 
-        def xt(h, kg):
-            words = xs[h][:].rearrange("p b d -> p (b d)").bitcast(F32).rearrange("p (b w) -> p b w", b=4)
+        def take_bank(name):
+            bank = free_banks.pop(0)
+            return bank, psum.tile([P, W], F32, tag=f"bank{bank}", name=name)
+
+        x_banks = {}
+
+        def turn_x(h, kg):
+            words = x_rows[h][:].rearrange("p b d -> p (b d)").bitcast(F32).rearrange("p (b w) -> p b w", b=CB)
             for pair in range(2):
-                bank = psum_o.tile([P, 2, 2 * P], F32, tag="o", name=f"xt_{h}_{kg}_{pair}")
-                xt_banks[h, kg, pair] = bank
-                for bb in range(2):
+                x_banks[h, kg, pair] = take_bank(f"xt_{h}_{kg}_{pair}")
+                bank = x_banks[h, kg, pair][1][:].rearrange("p (u q) -> p u q", u=2)
+                for b in range(2):
                     for u in range(2):
                         nc.tensor.transpose(
-                            bank[:, u, bb * P:(bb + 1) * P],
-                            words[:, 2 * pair + bb, 256 * kg + u:256 * (kg + 1):2],
-                            ident[:],
+                            bank[:, u, b * P:(b + 1) * P], words[:, 2 * pair + b, UNIT // 4 * kg + u:UNIT // 4 * (kg + 1):2], ident[:]
                         )
 
-        def xc(h, kg, who):
-            dst = mix_tile(("x", h, kg), W)
-            xw = dst[:].rearrange("p q e -> p (q e)").bitcast(F32).rearrange("p (q u) -> p q u", u=2)
-            for pair in range(2):
-                copy(who[pair], xw[:, 2 * pair * P:2 * (pair + 1) * P, :], xt_banks[h, kg, pair][:].rearrange("p u q -> p q u"))
+        def copy_x(h, kg, who):
+            dst = mixed_tile(("x", h, 0))[:].rearrange("p n e -> p (n e)").bitcast(F32).rearrange("p (q u) -> p q u", u=2)
+            for pair, engine in enumerate(who):
+                index, bank = x_banks[h, kg, pair]
+                lo = kg * W + pair * 2 * P
+                copy(engine, dst[:, lo:lo + 2 * P, :], bank[:].rearrange("p (u q) -> p q u", u=2))
+                free_banks.append(index)
+
+        def product(bank, left, left_cols, right, right_cols, start, stop):
+            nc.tensor.matmul_mx(
+                out=bank,
+                lhsT=codes[left][:, left_cols].bitcast(FP8X4),
+                lhsT_scale=scales[left][:, left_cols],
+                rhs=codes[right][:, right_cols].bitcast(FP8X4),
+                rhs_scale=scales[right][:, right_cols],
+                start=start,
+                stop=stop,
+            )
+
+        def place(c, g):
+            width = CHUNKS[c][1] * P
+            return ("e", c, g * width // UNIT), g * width % UNIT, width
 
         def stage1(c, g):
-            b0, nb = CHUNKS[c]
-            nq = nb * P
-            h, q0 = b0 // 4, (b0 % 4) * P
-            planes["e", c, g] = work.tile([P, 4, nq], BF16, tag=f"ep{nq}", bufs=3, name=f"ep_{c}_{g}")
+            unit, dst_lo, width = place(c, g)
+            dst = plane_tile(unit)
+            z_lo = g % 2 * W
+            half, first = CHUNKS[c][0] // CB, CHUNKS[c][0] % CB * P
             sums = {}
             for t in range(5):
                 if t < 4:
-                    sums[t] = psum_s.tile([P, nq], F32, tag="s", name=f"s_{c}_{g}_{t}")
+                    sums[t] = take_bank(f"s_{c}_{g}_{t}")
                     for kg in range(KG):
-                        zc, zp = quant["z", kg, g]
-                        xcod, xsc = quant["x", h, kg]
-                        nc.tensor.matmul_mx(
-                            out=sums[t][:],
-                            lhsT=zc[:, t * P:(t + 1) * P].bitcast(FP8X4),
-                            lhsT_scale=zp[:, t * P:(t + 1) * P],
-                            rhs=xcod[:, q0:q0 + nq].bitcast(FP8X4),
-                            rhs_scale=xsc[:, q0:q0 + nq],
-                            start=(kg == 0),
-                            stop=(kg == KG - 1),
+                        product(
+                            sums[t][1][:, :width], ("z", kg, g // 2), slice(z_lo + t * P, z_lo + (t + 1) * P),
+                            ("x", half, 0), slice(kg * W + first, kg * W + first + width), kg == 0, kg == KG - 1,
                         )
                 if t > 0:
-                    nc.scalar.activation(out=planes["e", c, g][:, t - 1, :], in_=sums[t - 1][:], func=ACT.Exp, bias=ln_az[:, 4 * g + t - 1:4 * g + t])
+                    index, bank = sums[t - 1]
+                    k = 4 * g + t - 1
+                    nc.scalar.activation(out=dst[:, t - 1, dst_lo:dst_lo + width], in_=bank[:, :width], func=ACT.Exp, bias=ln_az[:, k:k + 1])
+                    free_banks.append(index)
 
-        def ei(c, g, who):
-            mix(("e", c, g), who, CHUNKS[c][1] * P)
+        out_banks = {}
 
-        def eq(c, g):
-            q(("e", c, g), CHUNKS[c][1] * P)
-
-        banks = {}
-
-        def p_mm(c, b, gs, rs=range(RH)):
-            e0 = (b - CHUNKS[c][0]) * P
-            for r in rs:
-                if (b, r) not in banks:
-                    banks[b, r] = psum_o.tile([P, W], F32, tag="o", name=f"o_{b}_{r}")
-                for g in gs:
-                    ec, es = quant["e", c, g]
-                    ac, asc = quant["a", g, r]
-                    nc.tensor.matmul_mx(
-                        out=banks[b, r][:],
-                        lhsT=ec[:, e0:e0 + P].bitcast(FP8X4),
-                        lhsT_scale=es[:, e0:e0 + P],
-                        rhs=ac[:].bitcast(FP8X4),
-                        rhs_scale=asc[:],
-                        start=(g == 0),
-                        stop=(g == NG - 1),
-                    )
-
-        rows = {}
-        dst_rows = out.rearrange("(p b) r -> p b r", b=QB)
-
-        def fin(b, rs=range(RH)):
-            for r in rs:
-                rows[b, r] = res.tile([P, W], F32, tag="row", name=f"row_{b}_{r}")
-                cols = slice(r * W, (r + 1) * W)
-                nc.vector.scalar_tensor_tensor(
-                    out=rows[b, r][:], in0=banks[b, r][:], scalar=ax_in[:, b:b + 1], in1=off[:, cols], op0=ALU.mult, op1=ALU.add
+        def stage2(b, r, groups):
+            if (b, r) not in out_banks:
+                out_banks[b, r] = take_bank(f"o_{b}_{r}")
+            c = [i for i, (b0, nb) in enumerate(CHUNKS) if b0 <= b < b0 + nb][0]
+            for g in groups:
+                unit, lo, width = place(c, g)
+                lo += (b - CHUNKS[c][0]) * P
+                a_lo = g % 2 * W
+                product(
+                    out_banks[b, r][1][:], unit, slice(lo, lo + P), ("a", g // 2, r), slice(a_lo, a_lo + W), g == 0, g == NG - 1
                 )
-                nc.sync.dma_start(out=dst_rows[:, b, cols], in_=rows[b, r][:])
 
-        zw(0, 0, "SVSV")
-        zw(1, 0, "SSVV")
-        zi(0, 0, "V")
-        finish_logs()
-        xt(0, 1)
-        zi(1, 0, "SV")
-        q(("z", 0, 0))
-        q(("z", 1, 0))
-        zw(0, 1, "VVVV")
-        xc(0, 1, "SS")
-        xt(0, 0)
-        zw(1, 1, "VSVV")
-        zw(1, 2, "VSVS")
-        xt(1, 0)
-        xc(0, 0, "SS")
-        zw(0, 3, "VSVV")
-        q(("x", 0, 1))
-        zi(0, 1, "V")
-        q(("x", 0, 0))
-        zi(1, 1, "VS")
-        zi(1, 2, "VS")
-        xc(1, 0, "SV")
+        out_rows = out.rearrange("(p b) r -> p b r", b=QB)
+
+        def finish(b, r, who="V"):
+            index, bank = out_banks[b, r]
+            row = res.tile([P, W], F32, tag="row", name=f"row_{b}_{r}")
+            cols = slice(r * W, (r + 1) * W)
+            if who == "G":
+                scaled = res.tile([P, W], F32, tag="scaled", bufs=2, name=f"scaled_{b}_{r}")
+                nc.scalar.activation(out=scaled[:], in_=bank[:], func=ACT.Copy, scale=ax_f32[:, b:b + 1])
+                nc.gpsimd.tensor_tensor(out=row[:], in0=scaled[:], in1=off[:, cols], op=ALU.add)
+            else:
+                nc.vector.scalar_tensor_tensor(out=row[:], in0=bank[:], scalar=ax_in[:, b:b + 1], in1=off[:, cols], op0=ALU.mult, op1=ALU.add)
+            free_banks.append(index)
+            nc.sync.dma_start(out=out_rows[:, b, cols], in_=row[:])
+
+        take_logs()
+        widen_z(0, 0, "VVSVVVVV")
+        turn_x(0, 1)
+        widen_z(1, 0, "SSVSVSSV")
+        mix(("z", 0, 0), "VVVS")
+        mix(("z", 1, 0), "VV")
+        widen_z(0, 1, "SVVSSSSV")
+        copy_x(0, 1, "VS")
+        quantize(("z", 0, 0), 0, 1)
+        widen_z(1, 1, "VVVS")
+        turn_x(0, 0)
+        copy_x(0, 0, "SS")
+        turn_x(1, 1)
+        turn_x(1, 0)
+        quantize(("x", 0, 0), 0, 1)
+        quantize(("z", 1, 0), 0, 1)
+        mix(("z", 0, 1), "SVVV")
+        copy_x(1, 1, "SS")
+        copy_x(1, 0, "SS")
+        mix(("z", 1, 1), "SV")
         stage1(0, 0)
-        xt(1, 1)
-        xc(1, 1, "SS")
-        zw(1, 3, "VVVV")
-        q(("z", 0, 1))
-        q(("z", 1, 1))
-        zi(0, 3, "V")
-        q(("x", 1, 0))
-        zi(1, 3, "V")
-        zw(0, 2, "VVSV")
-        q(("x", 1, 1))
-        stage1(0, 1)
-        q(("z", 1, 2))
-        stage1(1, 1)
-        zi(0, 2, "V")
-        aw(0, 0, "VSSS")
-        q(("z", 0, 2))
-        ei(0, 0, "V")
-        stage1(1, 2)
-        q(("z", 0, 3))
-        q(("z", 1, 3))
-        stage1(1, 0)
-        stage1(0, 3)
-        ei(0, 1, "V")
-        ei(1, 2, "V")
-        eq(0, 1)
-        stage1(0, 2)
-        aw(2, 0, "VVSV")
-        aw(1, 0, "VSVS")
-        ei(1, 1, "V")
+        quantize(("z", 0, 1), 0, 1)
+        quantize(("z", 1, 1), 0, 1)
+        widen_a(0, 0, "SVSVSVVV")
+        quantize(("x", 1, 0), 0, 1)
         mix(("a", 0, 0), "V")
-        ei(0, 3, "V")
-        aw(3, 0, "VVVV")
-        mix(("a", 2, 0), "V")
-        stage1(1, 3)
-        mix(("a", 1, 0), "SV")
-        eq(1, 2)
-        eq(0, 0)
-        q(("a", 0, 0))
-        q(("a", 1, 0))
+        stage1(0, 1)
+        mix(("e", 0, 0), "V")
+        stage1(0, 2)
+        stage1(1, 2)
+        quantize(("a", 0, 0), 0, 1)
         stage1(2, 0)
-        ei(1, 0, "VS")
-        q(("a", 2, 0))
-        ei(0, 2, "SV")
-        mix(("a", 3, 0), "VS")
-        stage1(2, 1)
-        eq(0, 2)
-        aw(3, 1, "SSSS")
-        p_mm(0, 2, [0, 1], [0])
-        eq(0, 3)
-        p_mm(0, 1, [0, 1], [0])
-        q(("a", 3, 0))
-        p_mm(0, 0, [0, 1], [0])
-        p_mm(0, 3, [0, 1], [0])
-        p_mm(0, 0, [2], [0])
-        eq(1, 0)
-        p_mm(0, 3, [2], [0])
-        p_mm(0, 1, [2], [0])
-        p_mm(0, 2, [2], [0])
-        p_mm(0, 2, [3], [0])
-        eq(1, 1)
-        p_mm(0, 3, [3], [0])
-        aw(0, 1, "VVSV")
-        fin(2, [0])
-        ei(1, 3, "V")
-        p_mm(0, 1, [3], [0])
-        fin(1, [0])
-        eq(1, 3)
-        mix(("a", 0, 1), "V")
-        aw(1, 1, "VSSV")
-        p_mm(0, 0, [3], [0])
-        aw(2, 1, "VSSS")
-        mix(("a", 1, 1), "SV")
-        fin(0, [0])
+        stage1(1, 1)
+        quantize(("e", 0, 0), 0, 1)
+        widen_a(0, 1, "VVVVSVSS")
         stage1(2, 2)
-        p_mm(1, 5, [0, 1, 2, 3], [0])
-        mix(("a", 3, 1), "S")
-        ei(2, 0, "S")
-        fin(3, [0])
-        q(("a", 0, 1))
-        p_mm(1, 4, [0, 1, 2, 3], [0])
+        mix(("a", 0, 1), "VVVS")
+        stage2(1, 0, (0,))
+        stage2(2, 0, (0,))
+        stage2(2, 0, (1,))
+        stage2(1, 0, (1,))
+        stage1(1, 0)
+        widen_a(1, 1, "VVSSVVSV")
+        stage1(0, 3)
+        stage2(3, 0, (0,))
+        quantize(("a", 0, 1), 0, 1)
+        stage2(3, 0, (1,))
+        stage2(1, 1, (0,))
+        stage2(1, 1, (1,))
+        stage2(0, 1, (0,))
+        stage2(0, 1, (1,))
+        stage1(1, 3)
         stage1(2, 3)
-        q(("a", 1, 1))
-        mix(("a", 2, 1), "V")
-        fin(5, [0])
-        p_mm(0, 1, [0, 1], [1])
-        q(("a", 2, 1))
-        fin(4, [0])
-        p_mm(0, 2, [0, 1], [1])
-        q(("a", 3, 1))
-        p_mm(0, 3, [0, 1], [1])
-        ei(2, 1, "S")
-        ei(2, 2, "V")
-        p_mm(0, 2, [2], [1])
-        ei(2, 3, "S")
-        p_mm(0, 1, [2], [1])
-        p_mm(1, 5, [0, 1, 2, 3], [1])
-        eq(2, 0)
-        p_mm(0, 1, [3], [1])
-        p_mm(0, 2, [3], [1])
-        fin(1, [1])
-        fin(2, [1])
-        p_mm(0, 3, [2], [1])
-        p_mm(0, 3, [3], [1])
-        eq(2, 2)
-        fin(3, [1])
-        p_mm(0, 0, [0, 1], [1])
-        p_mm(0, 0, [2], [1])
-        p_mm(0, 0, [3], [1])
-        eq(2, 1)
-        p_mm(1, 4, [0, 1, 2, 3], [1])
-        fin(5, [1])
-        eq(2, 3)
-        p_mm(2, 7, [0, 1, 2, 3], [1])
-        fin(4, [1])
-        fin(0, [1])
-        p_mm(2, 6, [0, 1, 2, 3], [0])
-        fin(7, [1])
-        fin(6, [0])
-        p_mm(2, 7, [0, 1, 2, 3], [0])
-        fin(7, [0])
-        p_mm(2, 6, [0, 1, 2, 3], [1])
-        fin(6, [1])
+        stage1(2, 1)
+        widen_a(1, 0, "SVVVVVSV")
+        mix(("a", 1, 1), "V")
+        mix(("e", 0, 1), "V")
+        stage2(0, 0, (0,))
+        stage2(0, 0, (1,))
+        stage2(3, 1, (0,))
+        stage2(3, 1, (1,))
+        quantize(("a", 1, 1), 0, 1)
+        quantize(("e", 0, 1), 0, 1)
+        stage2(2, 1, (0,))
+        stage2(2, 1, (1,))
+        stage2(0, 1, (2,))
+        stage2(3, 1, (2,))
+        mix(("a", 1, 0), "SVVV")
+        stage2(1, 1, (2,))
+        stage2(2, 1, (2,))
+        stage2(3, 1, (3,))
+        quantize(("a", 1, 0), 0, 2)
+        stage2(2, 1, (3,))
+        stage2(0, 1, (3,))
+        stage2(1, 1, (3,))
+        stage2(3, 0, (2,))
+        stage2(1, 0, (2,))
+        quantize(("a", 1, 0), 1, 2)
+        mix(("e", 2, 0), "VSSS")
+        stage2(2, 0, (2,))
+        stage2(2, 0, (3,))
+        finish(2, 1)
+        stage2(1, 0, (3,))
+        quantize(("e", 2, 0), 0, 4)
+        stage2(3, 0, (3,))
+        quantize(("e", 2, 0), 1, 4)
+        stage2(0, 0, (2,))
+        stage2(0, 0, (3,))
+        quantize(("e", 2, 0), 2, 4)
+        stage2(6, 1, (0,))
+        finish(1, 0)
+        finish(3, 1)
+        quantize(("e", 2, 0), 3, 4)
+        stage2(6, 1, (1,))
+        finish(1, 1)
+        stage2(6, 1, (2,))
+        stage2(7, 0, (0,))
+        finish(3, 0)
+        stage2(7, 0, (1,))
+        stage2(7, 0, (2,))
+        stage2(6, 0, (0,))
+        stage2(7, 0, (3,))
+        stage2(6, 1, (3,))
+        stage2(6, 0, (1,))
+        finish(2, 0, "G")
+        stage2(7, 1, (0,))
+        stage2(7, 1, (1,))
+        stage2(7, 1, (2,))
+        mix(("e", 1, 0), "SS")
+        finish(0, 1)
+        quantize(("e", 1, 0), 0, 2)
+        stage2(7, 1, (3,))
+        stage2(6, 0, (2,))
+        stage2(6, 0, (3,))
+        finish(7, 0)
+        stage2(4, 1, (0,))
+        stage2(4, 0, (0,))
+        stage2(4, 0, (1,))
+        stage2(5, 1, (0,))
+        stage2(5, 0, (0,))
+        stage2(4, 1, (1,))
+        finish(0, 0)
+        finish(6, 1)
+        quantize(("e", 1, 0), 1, 2)
+        stage2(5, 1, (1,))
+        stage2(5, 0, (1,))
+        stage2(5, 1, (2,))
+        stage2(4, 0, (2,))
+        stage2(4, 0, (3,))
+        stage2(5, 0, (2,))
+        finish(6, 0)
+        finish(7, 1)
+        stage2(5, 1, (3,))
+        stage2(4, 1, (2,))
+        finish(4, 0)
+        stage2(4, 1, (3,))
+        finish(5, 1)
+        stage2(5, 0, (3,))
+        finish(4, 1)
+        finish(5, 0)

@@ -14,6 +14,7 @@ FP8 = mybir.dt.float8_e4m3fn
 FP8X4 = mybir.dt.float8_e4m3fn_x4
 ACT = mybir.ActivationFunctionType
 ALU = mybir.AluOpType
+AXES = mybir.AxisListType
 
 P = 128
 W = 512
@@ -21,8 +22,10 @@ UNIT = 2 * W
 KG = D // W
 NG = N // W
 QB = M // P
-CB = W // P
+HALF_QB = QB // 2
 CHUNKS = ((0, 4), (4, 2), (6, 2))
+BANKS = 8
+
 LN_EDGE = 2.0 ** 62
 LN_TOP = 2.0 ** 64
 LN_MIN = 2.0 ** -126
@@ -35,14 +38,14 @@ def tile_gp_mean_fp8_d5_kernel(tc, x, Z_bytes, Z_scale, A_bytes, A_scale, az, ax
         raw = ctx.enter_context(tc.tile_pool(name="raw", bufs=1))
         work = ctx.enter_context(tc.tile_pool(name="work", bufs=6))
         keep = ctx.enter_context(tc.tile_pool(name="keep", bufs=1))
-        res = ctx.enter_context(tc.tile_pool(name="res", bufs=6))
+        rows = ctx.enter_context(tc.tile_pool(name="rows", bufs=6))
         psum = ctx.enter_context(tc.psum_pool(name="psum", bufs=1))
         ctx.enter_context(tc.manual_schedule())
 
         az_in = const.tile([P, NG, 4], BF16, name="az_in")
         nc.scalar.dma_start(out=az_in[:], in_=az.rearrange("(g p t) -> p g t", p=P, t=4))
-        zs = const.tile([P, KG, 4], F32, name="zs")
-        nc.scalar.dma_start(out=zs[:], in_=Z_scale.rearrange("(g p t) o -> p g (t o)", p=P, t=4))
+        z_scale = const.tile([P, KG, 4], F32, name="z_scale")
+        nc.scalar.dma_start(out=z_scale[:], in_=Z_scale.rearrange("(g p t) o -> p g (t o)", p=P, t=4))
 
         z_src = Z_bytes.rearrange("(g p t) n -> g p t n", p=P, t=4)
         z_bytes = {(kg, h): raw.tile([P, 4, UNIT], U8, name=f"z_bytes_{kg}_{h}") for kg in range(KG) for h in range(2)}
@@ -51,20 +54,21 @@ def tile_gp_mean_fp8_d5_kernel(tc, x, Z_bytes, Z_scale, A_bytes, A_scale, az, ax
             nc.sync.dma_start(out=z_bytes[kg, h][:, :, lo:hi], in_=z_src[kg][:, :, h * UNIT + lo:h * UNIT + hi])
 
         x_src = x.rearrange("(p b) d -> p b d", b=QB)
-        x_rows = {h: raw.tile([P, CB, D], BF16, name=f"x_rows_{h}") for h in range(2)}
+        x_rows = {h: raw.tile([P, HALF_QB, D], BF16, name=f"x_rows_{h}") for h in range(2)}
 
         def load_x(h):
-            nc.sync.dma_start(out=x_rows[h][:], in_=x_src[:, CB * h:CB * (h + 1), :])
+            nc.sync.dma_start(out=x_rows[h][:], in_=x_src[:, HALF_QB * h:HALF_QB * (h + 1), :])
 
-        load_z(0, 0, 0, W)
+        for t in range(4):
+            nc.sync.dma_start(out=z_bytes[0, 0][:, t, 0:W], in_=z_src[0][:, t, 0:W])
         load_z(1, 0, 0, W)
         load_z(0, 0, W, UNIT)
         load_z(1, 0, W, UNIT)
         load_x(0)
         load_z(0, 1, 0, UNIT)
         load_z(1, 1, 0, UNIT)
-        as_in = const.tile([P, NG, 4], F32, name="as_in")
-        nc.sync.dma_start(out=as_in[:], in_=A_scale.rearrange("(g p t) o -> p g (t o)", p=P, t=4))
+        a_scale_in = const.tile([P, NG, 4], F32, name="a_scale_in")
+        nc.sync.dma_start(out=a_scale_in[:], in_=A_scale.rearrange("(g p t) o -> p g (t o)", p=P, t=4))
         load_x(1)
         a_src = A_bytes.rearrange("(g p t) n -> g p (t n)", p=P, t=4)
         a_bytes = {}
@@ -73,44 +77,55 @@ def tile_gp_mean_fp8_d5_kernel(tc, x, Z_bytes, Z_scale, A_bytes, A_scale, az, ax
             nc.sync.dma_start(out=a_bytes[g][:].rearrange("p t n -> p (t n)"), in_=a_src[g])
         ax_in = const.tile([P, QB], BF16, name="ax_in")
         nc.sync.dma_start(out=ax_in[:], in_=ax.rearrange("(p b) -> p b", b=QB))
-        off = const.tile([P, R], BF16, name="off")
-        nc.sync.dma_start(out=off[:], in_=offset.partition_broadcast(P))
+        offset_in = const.tile([P, R], BF16, name="offset_in")
+        nc.sync.dma_start(out=offset_in[:], in_=offset.partition_broadcast(P))
 
-        ident = const.tile([P, P], F32, name="ident")
-        make_identity(nc, ident[:])
+        identity = const.tile([P, P], F32, name="identity")
+        make_identity(nc, identity[:])
 
         az_flat = az_in[:].rearrange("p g t -> p (g t)")
-        az_abs = const.tile([P, NG * 4], F32, name="az_abs")
-        nc.vector.scalar_tensor_tensor(out=az_abs[:], in0=az_flat, scalar=-1.0, in1=az_flat, op0=ALU.mult, op1=ALU.max)
+        size = const.tile([P, NG * 4], F32, name="size")
+        step = const.tile([P, NG * 4], F32, name="step")
         low = const.tile([P, NG * 4], F32, name="low")
-        nc.vector.tensor_scalar(out=low[:], in0=az_abs[:], scalar1=LN_MIN, scalar2=LN_EDGE, op0=ALU.max, op1=ALU.mult)
-        parts = const.tile([P, 3, NG * 4], F32, name="parts")
-        nc.vector.tensor_scalar(out=parts[:, 0, :], in0=az_abs[:], scalar1=1.0 / LN_EDGE, scalar2=LN_TOP, op0=ALU.max, op1=ALU.min)
-        nc.vector.tensor_scalar(out=parts[:, 1, :], in0=az_abs[:], scalar1=1.0 / LN_TOP, scalar2=1.0, op0=ALU.mult, op1=ALU.max)
-        nc.vector.tensor_scalar(out=parts[:, 2, :], in0=low[:], scalar1=1.0, scalar2=1.0, op0=ALU.min, op1=ALU.mult)
-        az_step = const.tile([P, NG * 4], F32, name="az_step")
-        nc.gpsimd.tensor_scalar(out=az_step[:], in0=az_flat, scalar1=0.0, scalar2=2.0, op0=ALU.is_ge, op1=ALU.mult)
-        az_sign = const.tile([P, NG * 4], F32, name="az_sign")
-        nc.gpsimd.tensor_scalar(out=az_sign[:], in0=az_step[:], scalar1=-1.0, scalar2=1.0, op0=ALU.add, op1=ALU.mult)
+        factors = const.tile([P, 3, NG * 4], F32, name="factors")
+        nc.vector.scalar_tensor_tensor(out=size[:], in0=az_flat, scalar=-1.0, in1=az_flat, op0=ALU.mult, op1=ALU.max)
+        nc.vector.tensor_scalar(out=step[:], in0=az_flat, scalar1=0.0, scalar2=2.0, op0=ALU.is_ge, op1=ALU.mult)
+        nc.vector.tensor_scalar(out=low[:], in0=size[:], scalar1=LN_MIN, scalar2=LN_EDGE, op0=ALU.max, op1=ALU.mult)
+        nc.vector.tensor_scalar(out=factors[:, 0, :], in0=size[:], scalar1=1.0 / LN_EDGE, scalar2=LN_TOP, op0=ALU.max, op1=ALU.min)
+        nc.vector.tensor_scalar(out=factors[:, 1, :], in0=size[:], scalar1=1.0 / LN_TOP, scalar2=1.0, op0=ALU.mult, op1=ALU.max)
+        nc.vector.tensor_scalar(out=factors[:, 2, :], in0=low[:], scalar1=1.0, scalar2=None, op0=ALU.min)
         logs = const.tile([P, 3, NG * 4], F32, name="logs")
-        ln_two = const.tile([P, NG * 4], F32, name="ln_two")
         ln_az = const.tile([P, NG * 4], F32, name="ln_az")
         a_scale = const.tile([P, NG * 4], F32, name="a_scale")
 
-        ax_f32 = const.tile([P, QB], F32, name="ax_f32")
-
         def take_logs():
-            nc.scalar.activation(out=logs[:], in_=parts[:], func=ACT.Ln)
-            nc.gpsimd.tensor_tensor(out=ln_two[:], in0=logs[:, 0, :], in1=logs[:, 1, :], op=ALU.add)
-            nc.gpsimd.tensor_tensor(out=ln_az[:], in0=ln_two[:], in1=logs[:, 2, :], op=ALU.add)
-            nc.gpsimd.tensor_tensor(out=a_scale[:], in0=as_in[:].rearrange("p g t -> p (g t)"), in1=az_sign[:], op=ALU.mult)
-            nc.gpsimd.tensor_copy(out=ax_f32[:], in_=ax_in[:])
+            nc.scalar.activation(out=logs[:], in_=factors[:], func=ACT.Ln)
 
-        def widen(engine, dst, src, scale):
-            if engine == "S":
-                nc.scalar.activation(out=dst, in_=src.bitcast(FP8), func=ACT.Copy, scale=scale)
-            else:
-                nc.vector.tensor_scalar(out=dst, in0=src.bitcast(FP8), scalar1=scale, scalar2=None, op0=ALU.mult)
+        def add_logs():
+            nc.vector.tensor_reduce(out=ln_az[:], in_=logs[:].rearrange("p f n -> p n f"), op=ALU.add, axis=AXES.X)
+
+        def sign_a_scale():
+            nc.vector.scalar_tensor_tensor(
+                out=a_scale[:], in0=step[:], scalar=-1.0, in1=a_scale_in[:].rearrange("p g t -> p (g t)"), op0=ALU.add, op1=ALU.mult
+            )
+
+        planes = {}
+        mixed = {}
+        codes = {}
+        scales = {}
+
+        def unit_name(unit):
+            return "_".join(str(part) for part in unit)
+
+        def planes_of(unit):
+            if unit not in planes:
+                planes[unit] = work.tile([P, 4, UNIT], BF16, tag="planes", name="planes_" + unit_name(unit))
+            return planes[unit]
+
+        def mixed_of(unit):
+            if unit not in mixed:
+                mixed[unit] = work.tile([P, UNIT, 4], BF16, tag="mixed", name="mixed_" + unit_name(unit), align_bytes=64)
+            return mixed[unit]
 
         def copy(engine, dst, src):
             if engine == "S":
@@ -118,91 +133,84 @@ def tile_gp_mean_fp8_d5_kernel(tc, x, Z_bytes, Z_scale, A_bytes, A_scale, az, ax
             else:
                 nc.vector.tensor_copy(out=dst, in_=src)
 
-        planes = {}
-        mixed = {}
-        codes = {}
-        scales = {}
-
-        def plane_tile(unit):
-            if unit not in planes:
-                planes[unit] = work.tile([P, 4, UNIT], BF16, tag="planes", name="planes_" + "_".join(str(v) for v in unit))
-            return planes[unit]
-
-        def mixed_tile(unit):
-            if unit not in mixed:
-                mixed[unit] = work.tile([P, UNIT, 4], BF16, tag="mixed", name="mixed_" + "_".join(str(v) for v in unit), align_bytes=64)
-            return mixed[unit]
+        def widen(engine, dst, src, scale):
+            if engine == "S":
+                nc.scalar.activation(out=dst, in_=src.bitcast(FP8), func=ACT.Copy, scale=scale)
+            else:
+                nc.vector.tensor_scalar(out=dst, in0=src.bitcast(FP8), scalar1=scale, scalar2=None, op0=ALU.mult)
 
         def widen_z(kg, h, who):
-            dst = plane_tile(("z", kg, h))
-            step = 4 * UNIT // len(who)
+            dst = planes_of(("z", kg, h))
+            width = 4 * UNIT // len(who)
             for i, engine in enumerate(who):
-                t, lo = i % 4, i // 4 * step
-                widen(engine, dst[:, t, lo:lo + step], z_bytes[kg, h][:, t, lo:lo + step], zs[:, kg, t:t + 1])
+                t, lo = i % 4, i // 4 * width
+                widen(engine, dst[:, t, lo:lo + width], z_bytes[kg, h][:, t, lo:lo + width], z_scale[:, kg, t:t + 1])
 
         def widen_a(pair, r, who):
-            dst = plane_tile(("a", pair, r))
+            dst = planes_of(("a", pair, r))
             for i, engine in enumerate(who):
-                t, half = i % 4, i // 4
-                g = 2 * pair + half
-                widen(engine, dst[:, t, half * W:(half + 1) * W], a_bytes[g][:, t, r * W:(r + 1) * W], a_scale[:, 4 * g + t:4 * g + t + 1])
+                t, g = i % 4, 2 * pair + i // 4
+                lo = i // 4 * W
+                widen(engine, dst[:, t, lo:lo + W], a_bytes[g][:, t, r * W:(r + 1) * W], a_scale[:, 4 * g + t:4 * g + t + 1])
 
         def mix(unit, who):
-            dst, src = mixed_tile(unit), planes[unit]
-            step = UNIT // len(who)
+            dst, src = mixed_of(unit), planes[unit]
+            width = UNIT // len(who)
             for i, engine in enumerate(who):
-                lo = i * step
+                lo = i * width
+                piece = dst[:, lo:lo + width, :]
                 if unit[0] == "z":
-                    half, t0, tiles = lo // W, lo % W // P, step // P
-                    copy(engine,
-                         dst[:, lo:lo + step, :].rearrange("p (t c i) j -> p t c j i", t=tiles, i=4),
-                         src[:, :, half * W:(half + 1) * W].rearrange("p j (c i t) -> p t c j i", i=4, t=4)[:, t0:t0 + tiles])
+                    group, t0, tiles = lo // W * W, lo % W // P, width // P
+                    by_tile = src[:, :, group:group + W].rearrange("p j (c i t) -> p t c j i", i=4, t=4)
+                    copy(engine, piece.rearrange("p (t c i) j -> p t c j i", t=tiles, i=4), by_tile[:, t0:t0 + tiles])
                 else:
-                    copy(engine,
-                         dst[:, lo:lo + step, :].rearrange("p (c i) t -> p c t i", i=4),
-                         src[:, :, lo:lo + step].rearrange("p t (c i) -> p c t i", i=4))
+                    columns = src[:, :, lo:lo + width].rearrange("p t (c i) -> p c t i", i=4)
+                    copy(engine, piece.rearrange("p (c i) t -> p c t i", i=4), columns)
 
-        def quantize(unit, part, parts_in_all):
-            name = "_".join(str(v) for v in unit)
+        def quantize(unit, part, parts):
             if unit not in codes:
-                codes[unit] = keep.tile([P, UNIT], U32, name=f"codes_{name}", align_bytes=64)
-                scales[unit] = keep.tile([P, UNIT], U8, name=f"scales_{name}", align_bytes=64)
-            step = UNIT // parts_in_all
-            cols = slice(part * step, (part + 1) * step)
+                codes[unit] = keep.tile([P, UNIT], U32, name="codes_" + unit_name(unit), align_bytes=64)
+                scales[unit] = keep.tile([P, UNIT], U8, name="scales_" + unit_name(unit), align_bytes=64)
+            width = UNIT // parts
+            cols = slice(part * width, (part + 1) * width)
             nc.vector.quantize_mx(
-                out=codes[unit][:, cols].bitcast(FP8X4), scales=scales[unit][:, cols], in_=mixed[unit][:, cols, :].rearrange("p n t -> p (n t)")
+                out=codes[unit][:, cols].bitcast(FP8X4),
+                scales=scales[unit][:, cols],
+                in_=mixed[unit][:, cols, :].rearrange("p n t -> p (n t)"),
             )
 
-        free_banks = list(range(8))
+        free_banks = list(range(BANKS))
 
         def take_bank(name):
-            bank = free_banks.pop(0)
-            return bank, psum.tile([P, W], F32, tag=f"bank{bank}", name=name)
+            index = free_banks.pop(0)
+            return index, psum.tile([P, W], F32, tag=f"bank{index}", name=name)
 
         x_banks = {}
 
         def turn_x(h, kg):
-            words = x_rows[h][:].rearrange("p b d -> p (b d)").bitcast(F32).rearrange("p (b w) -> p b w", b=CB)
+            words = x_rows[h][:].rearrange("p b d -> p (b d)").bitcast(F32).rearrange("p (b w) -> p b w", b=HALF_QB)
             for pair in range(2):
-                x_banks[h, kg, pair] = take_bank(f"xt_{h}_{kg}_{pair}")
-                bank = x_banks[h, kg, pair][1][:].rearrange("p (u q) -> p u q", u=2)
+                x_banks[h, kg, pair] = take_bank(f"x_turned_{h}_{kg}_{pair}")
+                turned = x_banks[h, kg, pair][1][:].rearrange("p (u q) -> p u q", u=2)
                 for b in range(2):
                     for u in range(2):
                         nc.tensor.transpose(
-                            bank[:, u, b * P:(b + 1) * P], words[:, 2 * pair + b, UNIT // 4 * kg + u:UNIT // 4 * (kg + 1):2], ident[:]
+                            turned[:, u, b * P:(b + 1) * P],
+                            words[:, 2 * pair + b, W // 2 * kg + u:W // 2 * (kg + 1):2],
+                            identity[:],
                         )
 
         def copy_x(h, kg, who):
-            dst = mixed_tile(("x", h, 0))[:].rearrange("p n e -> p (n e)").bitcast(F32).rearrange("p (q u) -> p q u", u=2)
+            dst = mixed_of(("x", h, 0))[:].rearrange("p n e -> p (n e)").bitcast(F32).rearrange("p (q u) -> p q u", u=2)
             for pair, engine in enumerate(who):
                 index, bank = x_banks[h, kg, pair]
                 lo = kg * W + pair * 2 * P
                 copy(engine, dst[:, lo:lo + 2 * P, :], bank[:].rearrange("p (u q) -> p q u", u=2))
                 free_banks.append(index)
 
-        def product(bank, left, left_cols, right, right_cols, start, stop):
+        def product(sums, left, left_cols, right, right_cols, start, stop):
             nc.tensor.matmul_mx(
-                out=bank,
+                out=sums,
                 lhsT=codes[left][:, left_cols].bitcast(FP8X4),
                 lhsT_scale=scales[left][:, left_cols],
                 rhs=codes[right][:, right_cols].bitcast(FP8X4),
@@ -216,191 +224,194 @@ def tile_gp_mean_fp8_d5_kernel(tc, x, Z_bytes, Z_scale, A_bytes, A_scale, az, ax
             return ("e", c, g * width // UNIT), g * width % UNIT, width
 
         def stage1(c, g):
-            unit, dst_lo, width = place(c, g)
-            dst = plane_tile(unit)
+            unit, lo, width = place(c, g)
+            dst = planes_of(unit)
             z_lo = g % 2 * W
-            half, first = CHUNKS[c][0] // CB, CHUNKS[c][0] % CB * P
-            sums = {}
+            half, first = CHUNKS[c][0] // HALF_QB, CHUNKS[c][0] % HALF_QB * P
+            tiles = {}
             for t in range(5):
                 if t < 4:
-                    sums[t] = take_bank(f"s_{c}_{g}_{t}")
+                    tiles[t] = take_bank(f"s_{c}_{g}_{t}")
                     for kg in range(KG):
                         product(
-                            sums[t][1][:, :width], ("z", kg, g // 2), slice(z_lo + t * P, z_lo + (t + 1) * P),
-                            ("x", half, 0), slice(kg * W + first, kg * W + first + width), kg == 0, kg == KG - 1,
+                            tiles[t][1][:, :width],
+                            ("z", kg, g // 2), slice(z_lo + t * P, z_lo + (t + 1) * P),
+                            ("x", half, 0), slice(kg * W + first, kg * W + first + width),
+                            kg == 0, kg == KG - 1,
                         )
                 if t > 0:
-                    index, bank = sums[t - 1]
-                    k = 4 * g + t - 1
-                    nc.scalar.activation(out=dst[:, t - 1, dst_lo:dst_lo + width], in_=bank[:, :width], func=ACT.Exp, bias=ln_az[:, k:k + 1])
+                    index, bank = tiles[t - 1]
+                    column = 4 * g + t - 1
+                    nc.scalar.activation(
+                        out=dst[:, t - 1, lo:lo + width], in_=bank[:, :width], func=ACT.Exp, bias=ln_az[:, column:column + 1]
+                    )
                     free_banks.append(index)
 
         out_banks = {}
 
         def stage2(b, r, groups):
             if (b, r) not in out_banks:
-                out_banks[b, r] = take_bank(f"o_{b}_{r}")
-            c = [i for i, (b0, nb) in enumerate(CHUNKS) if b0 <= b < b0 + nb][0]
+                out_banks[b, r] = take_bank(f"p_{b}_{r}")
+            c = [i for i, (first, count) in enumerate(CHUNKS) if first <= b < first + count][0]
             for g in groups:
-                unit, lo, width = place(c, g)
-                lo += (b - CHUNKS[c][0]) * P
+                unit, lo = place(c, g)[:2]
+                e_lo = lo + (b - CHUNKS[c][0]) * P
                 a_lo = g % 2 * W
                 product(
-                    out_banks[b, r][1][:], unit, slice(lo, lo + P), ("a", g // 2, r), slice(a_lo, a_lo + W), g == 0, g == NG - 1
+                    out_banks[b, r][1][:], unit, slice(e_lo, e_lo + P), ("a", g // 2, r), slice(a_lo, a_lo + W), g == 0, g == NG - 1
                 )
 
         out_rows = out.rearrange("(p b) r -> p b r", b=QB)
 
-        def finish(b, r, who="V"):
+        def finish(b, r):
             index, bank = out_banks[b, r]
-            row = res.tile([P, W], F32, tag="row", name=f"row_{b}_{r}")
+            row = rows.tile([P, W], F32, tag="row", name=f"row_{b}_{r}")
             cols = slice(r * W, (r + 1) * W)
-            if who == "G":
-                scaled = res.tile([P, W], F32, tag="scaled", bufs=2, name=f"scaled_{b}_{r}")
-                nc.scalar.activation(out=scaled[:], in_=bank[:], func=ACT.Copy, scale=ax_f32[:, b:b + 1])
-                nc.gpsimd.tensor_tensor(out=row[:], in0=scaled[:], in1=off[:, cols], op=ALU.add)
-            else:
-                nc.vector.scalar_tensor_tensor(out=row[:], in0=bank[:], scalar=ax_in[:, b:b + 1], in1=off[:, cols], op0=ALU.mult, op1=ALU.add)
+            nc.vector.scalar_tensor_tensor(
+                out=row[:], in0=bank[:], scalar=ax_in[:, b:b + 1], in1=offset_in[:, cols], op0=ALU.mult, op1=ALU.add
+            )
             free_banks.append(index)
             nc.sync.dma_start(out=out_rows[:, b, cols], in_=row[:])
 
-        take_logs()
-        widen_z(0, 0, "VVSVVVVV")
-        turn_x(0, 1)
-        widen_z(1, 0, "SSVSVSSV")
-        mix(("z", 0, 0), "VVVS")
-        mix(("z", 1, 0), "VV")
-        widen_z(0, 1, "SVVSSSSV")
-        copy_x(0, 1, "VS")
-        quantize(("z", 0, 0), 0, 1)
-        widen_z(1, 1, "VVVS")
         turn_x(0, 0)
+        turn_x(0, 1)
+        take_logs()
+        add_logs()
+        widen_z(0, 0, "SVVSVVVV")
+        widen_z(1, 0, "SSVSVSSV")
+        mix(("z", 1, 0), "VV")
+        turn_x(1, 0)
+        mix(("z", 0, 0), "VVVS")
+        widen_z(0, 1, "SVSSSVSV")
+        copy_x(0, 1, "SS")
+        quantize(("z", 0, 0), 0, 1)
         copy_x(0, 0, "SS")
         turn_x(1, 1)
-        turn_x(1, 0)
         quantize(("x", 0, 0), 0, 1)
         quantize(("z", 1, 0), 0, 1)
-        mix(("z", 0, 1), "SVVV")
-        copy_x(1, 1, "SS")
+        mix(("z", 0, 1), "VVVS")
         copy_x(1, 0, "SS")
-        mix(("z", 1, 1), "SV")
-        stage1(0, 0)
-        quantize(("z", 0, 1), 0, 1)
-        quantize(("z", 1, 1), 0, 1)
-        widen_a(0, 0, "SVSVSVVV")
+        copy_x(1, 1, "SS")
         quantize(("x", 1, 0), 0, 1)
-        mix(("a", 0, 0), "V")
+        widen_z(1, 1, "VVVS")
+        sign_a_scale()
+        stage1(0, 0)
+        mix(("z", 1, 1), "VS")
+        quantize(("z", 0, 1), 0, 1)
+        widen_a(0, 0, "VVVVVVSV")
         stage1(0, 1)
-        mix(("e", 0, 0), "V")
-        stage1(0, 2)
-        stage1(1, 2)
-        quantize(("a", 0, 0), 0, 1)
-        stage1(2, 0)
-        stage1(1, 1)
-        quantize(("e", 0, 0), 0, 1)
-        widen_a(0, 1, "VVVVSVSS")
-        stage1(2, 2)
-        mix(("a", 0, 1), "VVVS")
-        stage2(1, 0, (0,))
-        stage2(2, 0, (0,))
-        stage2(2, 0, (1,))
-        stage2(1, 0, (1,))
-        stage1(1, 0)
-        widen_a(1, 1, "VVSSVVSV")
-        stage1(0, 3)
-        stage2(3, 0, (0,))
-        quantize(("a", 0, 1), 0, 1)
-        stage2(3, 0, (1,))
-        stage2(1, 1, (0,))
-        stage2(1, 1, (1,))
-        stage2(0, 1, (0,))
-        stage2(0, 1, (1,))
-        stage1(1, 3)
-        stage1(2, 3)
         stage1(2, 1)
-        widen_a(1, 0, "SVVVVVSV")
+        quantize(("z", 1, 1), 0, 1)
+        mix(("a", 0, 0), "V")
+        stage1(1, 1)
+        stage1(2, 3)
+        stage1(1, 3)
+        mix(("e", 0, 0), "V")
+        stage1(0, 3)
+        quantize(("a", 0, 0), 0, 1)
+        quantize(("e", 0, 0), 0, 1)
+        widen_a(0, 1, "VVSVVVSS")
+        widen_a(1, 1, "SVVSVSVV")
+        mix(("a", 0, 1), "SVVV")
+        stage1(0, 2)
+        stage2(3, 0, (0,))
         mix(("a", 1, 1), "V")
-        mix(("e", 0, 1), "V")
+        stage2(3, 0, (1,))
+        stage2(2, 0, (0,))
+        quantize(("a", 0, 1), 0, 1)
+        quantize(("a", 1, 1), 0, 1)
         stage2(0, 0, (0,))
+        stage2(1, 0, (0,))
+        stage2(1, 0, (1,))
+        stage2(2, 0, (1,))
         stage2(0, 0, (1,))
+        stage1(1, 2)
+        stage1(1, 0)
+        stage1(2, 2)
+        stage1(2, 0)
         stage2(3, 1, (0,))
         stage2(3, 1, (1,))
-        quantize(("a", 1, 1), 0, 1)
-        quantize(("e", 0, 1), 0, 1)
+        mix(("e", 0, 1), "V")
         stage2(2, 1, (0,))
+        widen_a(1, 0, "SVVSVSSS")
+        stage2(1, 1, (0,))
+        quantize(("e", 0, 1), 0, 1)
+        stage2(0, 1, (0,))
+        stage2(1, 1, (1,))
         stage2(2, 1, (1,))
-        stage2(0, 1, (2,))
+        stage2(0, 1, (1,))
+        mix(("a", 1, 0), "VVVS")
         stage2(3, 1, (2,))
-        mix(("a", 1, 0), "SVVV")
-        stage2(1, 1, (2,))
-        stage2(2, 1, (2,))
         stage2(3, 1, (3,))
         quantize(("a", 1, 0), 0, 2)
-        stage2(2, 1, (3,))
-        stage2(0, 1, (3,))
-        stage2(1, 1, (3,))
-        stage2(3, 0, (2,))
-        stage2(1, 0, (2,))
-        quantize(("a", 1, 0), 1, 2)
+        stage2(2, 1, (2,))
+        stage2(1, 1, (2,))
         mix(("e", 2, 0), "VSSS")
-        stage2(2, 0, (2,))
-        stage2(2, 0, (3,))
-        finish(2, 1)
-        stage2(1, 0, (3,))
+        quantize(("a", 1, 0), 1, 2)
+        stage2(2, 1, (3,))
+        stage2(0, 1, (2,))
         quantize(("e", 2, 0), 0, 4)
-        stage2(3, 0, (3,))
-        quantize(("e", 2, 0), 1, 4)
-        stage2(0, 0, (2,))
-        stage2(0, 0, (3,))
-        quantize(("e", 2, 0), 2, 4)
-        stage2(6, 1, (0,))
-        finish(1, 0)
+        stage2(0, 1, (3,))
         finish(3, 1)
-        quantize(("e", 2, 0), 3, 4)
-        stage2(6, 1, (1,))
+        stage2(1, 1, (3,))
+        quantize(("e", 2, 0), 1, 4)
+        finish(2, 1)
+        stage2(0, 0, (2,))
+        stage2(1, 0, (2,))
+        stage2(3, 0, (2,))
+        stage2(2, 0, (2,))
         finish(1, 1)
-        stage2(6, 1, (2,))
-        stage2(7, 0, (0,))
-        finish(3, 0)
-        stage2(7, 0, (1,))
-        stage2(7, 0, (2,))
-        stage2(6, 0, (0,))
-        stage2(7, 0, (3,))
-        stage2(6, 1, (3,))
-        stage2(6, 0, (1,))
-        finish(2, 0, "G")
-        stage2(7, 1, (0,))
-        stage2(7, 1, (1,))
-        stage2(7, 1, (2,))
         mix(("e", 1, 0), "SS")
-        finish(0, 1)
-        quantize(("e", 1, 0), 0, 2)
-        stage2(7, 1, (3,))
+        stage2(2, 0, (3,))
+        stage2(1, 0, (3,))
+        quantize(("e", 2, 0), 2, 4)
+        stage2(0, 0, (3,))
+        stage2(3, 0, (3,))
+        stage2(6, 0, (0,))
+        stage2(6, 0, (1,))
+        finish(1, 0)
+        stage2(7, 0, (0,))
+        stage2(7, 0, (1,))
+        stage2(7, 1, (0,))
+        quantize(("e", 2, 0), 3, 4)
+        finish(2, 0)
+        stage2(7, 1, (1,))
         stage2(6, 0, (2,))
-        stage2(6, 0, (3,))
+        stage2(7, 1, (2,))
+        stage2(6, 1, (0,))
+        stage2(6, 1, (1,))
+        finish(3, 0)
+        finish(0, 1)
+        stage2(7, 0, (2,))
+        stage2(7, 0, (3,))
+        quantize(("e", 1, 0), 0, 2)
         finish(7, 0)
+        finish(0, 0)
+        stage2(6, 1, (2,))
+        stage2(7, 1, (3,))
+        stage2(6, 0, (3,))
+        stage2(6, 1, (3,))
         stage2(4, 1, (0,))
         stage2(4, 0, (0,))
         stage2(4, 0, (1,))
-        stage2(5, 1, (0,))
         stage2(5, 0, (0,))
         stage2(4, 1, (1,))
-        finish(0, 0)
-        finish(6, 1)
-        quantize(("e", 1, 0), 1, 2)
-        stage2(5, 1, (1,))
-        stage2(5, 0, (1,))
-        stage2(5, 1, (2,))
-        stage2(4, 0, (2,))
-        stage2(4, 0, (3,))
-        stage2(5, 0, (2,))
         finish(6, 0)
+        quantize(("e", 1, 0), 1, 2)
+        stage2(5, 0, (1,))
+        stage2(5, 1, (0,))
+        stage2(5, 1, (1,))
         finish(7, 1)
-        stage2(5, 1, (3,))
-        stage2(4, 1, (2,))
+        stage2(4, 0, (2,))
+        finish(6, 1)
+        stage2(4, 0, (3,))
         finish(4, 0)
+        stage2(4, 1, (2,))
+        stage2(5, 0, (2,))
         stage2(4, 1, (3,))
-        finish(5, 1)
-        stage2(5, 0, (3,))
         finish(4, 1)
+        stage2(5, 1, (2,))
+        stage2(5, 0, (3,))
         finish(5, 0)
+        stage2(5, 1, (3,))
+        finish(5, 1)

from contextlib import ExitStack

import concourse.mybir as mybir
from concourse.masks import make_identity

M, D, N, R = 1024, 1024, 2048, 1024
FLOPS = 2 * M * D * N + 2 * M * N * R

F32 = mybir.dt.float32
BF16 = mybir.dt.bfloat16
U32 = mybir.dt.uint32
U8 = mybir.dt.uint8
FP8 = mybir.dt.float8_e4m3fn
FP8X4 = mybir.dt.float8_e4m3fn_x4
ACT = mybir.ActivationFunctionType
ALU = mybir.AluOpType
AXES = mybir.AxisListType

P = 128
W = 512
UNIT = 2 * W
KG = D // W
NG = N // W
QB = M // P
HALF_QB = QB // 2
CHUNKS = ((0, 4), (4, 2), (6, 2))
BANKS = 8

LN_EDGE = 2.0 ** 62
LN_TOP = 2.0 ** 64
LN_MIN = 2.0 ** -126


def tile_gp_mean_fp8_d5_kernel(tc, x, Z_bytes, Z_scale, A_bytes, A_scale, az, ax, offset, out):
    nc = tc.nc
    with ExitStack() as ctx:
        const = ctx.enter_context(tc.tile_pool(name="const", bufs=1))
        raw = ctx.enter_context(tc.tile_pool(name="raw", bufs=1))
        work = ctx.enter_context(tc.tile_pool(name="work", bufs=6))
        keep = ctx.enter_context(tc.tile_pool(name="keep", bufs=1))
        rows = ctx.enter_context(tc.tile_pool(name="rows", bufs=6))
        psum = ctx.enter_context(tc.psum_pool(name="psum", bufs=1))
        ctx.enter_context(tc.manual_schedule())

        az_in = const.tile([P, NG, 4], BF16, name="az_in")
        nc.scalar.dma_start(out=az_in[:], in_=az.rearrange("(g p t) -> p g t", p=P, t=4))
        z_scale = const.tile([P, KG, 4], F32, name="z_scale")
        nc.scalar.dma_start(out=z_scale[:], in_=Z_scale.rearrange("(g p t) o -> p g (t o)", p=P, t=4))

        z_src = Z_bytes.rearrange("(g p t) n -> g p t n", p=P, t=4)
        z_bytes = {(kg, h): raw.tile([P, 4, UNIT], U8, name=f"z_bytes_{kg}_{h}") for kg in range(KG) for h in range(2)}

        def load_z(kg, h, lo, hi):
            nc.sync.dma_start(out=z_bytes[kg, h][:, :, lo:hi], in_=z_src[kg][:, :, h * UNIT + lo:h * UNIT + hi])

        x_src = x.rearrange("(p b) d -> p b d", b=QB)
        x_rows = {h: raw.tile([P, HALF_QB, D], BF16, name=f"x_rows_{h}") for h in range(2)}

        def load_x(h):
            nc.sync.dma_start(out=x_rows[h][:], in_=x_src[:, HALF_QB * h:HALF_QB * (h + 1), :])

        for t in range(4):
            nc.sync.dma_start(out=z_bytes[0, 0][:, t, 0:W], in_=z_src[0][:, t, 0:W])
        load_z(1, 0, 0, W)
        load_z(0, 0, W, UNIT)
        load_z(1, 0, W, UNIT)
        load_x(0)
        load_z(0, 1, 0, UNIT)
        load_z(1, 1, 0, UNIT)
        a_scale_in = const.tile([P, NG, 4], F32, name="a_scale_in")
        nc.sync.dma_start(out=a_scale_in[:], in_=A_scale.rearrange("(g p t) o -> p g (t o)", p=P, t=4))
        load_x(1)
        a_src = A_bytes.rearrange("(g p t) n -> g p (t n)", p=P, t=4)
        a_bytes = {}
        for g in range(NG):
            a_bytes[g] = raw.tile([P, 4, R], U8, name=f"a_bytes_{g}")
            nc.sync.dma_start(out=a_bytes[g][:].rearrange("p t n -> p (t n)"), in_=a_src[g])
        ax_in = const.tile([P, QB], BF16, name="ax_in")
        nc.sync.dma_start(out=ax_in[:], in_=ax.rearrange("(p b) -> p b", b=QB))
        offset_in = const.tile([P, R], BF16, name="offset_in")
        nc.sync.dma_start(out=offset_in[:], in_=offset.partition_broadcast(P))

        identity = const.tile([P, P], F32, name="identity")
        make_identity(nc, identity[:])

        az_flat = az_in[:].rearrange("p g t -> p (g t)")
        size = const.tile([P, NG * 4], F32, name="size")
        step = const.tile([P, NG * 4], F32, name="step")
        low = const.tile([P, NG * 4], F32, name="low")
        factors = const.tile([P, 3, NG * 4], F32, name="factors")
        nc.vector.scalar_tensor_tensor(out=size[:], in0=az_flat, scalar=-1.0, in1=az_flat, op0=ALU.mult, op1=ALU.max)
        nc.vector.tensor_scalar(out=step[:], in0=az_flat, scalar1=0.0, scalar2=2.0, op0=ALU.is_ge, op1=ALU.mult)
        nc.vector.tensor_scalar(out=low[:], in0=size[:], scalar1=LN_MIN, scalar2=LN_EDGE, op0=ALU.max, op1=ALU.mult)
        nc.vector.tensor_scalar(out=factors[:, 0, :], in0=size[:], scalar1=1.0 / LN_EDGE, scalar2=LN_TOP, op0=ALU.max, op1=ALU.min)
        nc.vector.tensor_scalar(out=factors[:, 1, :], in0=size[:], scalar1=1.0 / LN_TOP, scalar2=1.0, op0=ALU.mult, op1=ALU.max)
        nc.vector.tensor_scalar(out=factors[:, 2, :], in0=low[:], scalar1=1.0, scalar2=None, op0=ALU.min)
        logs = const.tile([P, 3, NG * 4], F32, name="logs")
        ln_az = const.tile([P, NG * 4], F32, name="ln_az")
        a_scale = const.tile([P, NG * 4], F32, name="a_scale")

        def take_logs():
            nc.scalar.activation(out=logs[:], in_=factors[:], func=ACT.Ln)

        def add_logs():
            nc.vector.tensor_reduce(out=ln_az[:], in_=logs[:].rearrange("p f n -> p n f"), op=ALU.add, axis=AXES.X)

        def sign_a_scale():
            nc.vector.scalar_tensor_tensor(
                out=a_scale[:], in0=step[:], scalar=-1.0, in1=a_scale_in[:].rearrange("p g t -> p (g t)"), op0=ALU.add, op1=ALU.mult
            )

        planes = {}
        mixed = {}
        codes = {}
        scales = {}

        def unit_name(unit):
            return "_".join(str(part) for part in unit)

        def planes_of(unit):
            if unit not in planes:
                planes[unit] = work.tile([P, 4, UNIT], BF16, tag="planes", name="planes_" + unit_name(unit))
            return planes[unit]

        def mixed_of(unit):
            if unit not in mixed:
                mixed[unit] = work.tile([P, UNIT, 4], BF16, tag="mixed", name="mixed_" + unit_name(unit), align_bytes=64)
            return mixed[unit]

        def copy(engine, dst, src):
            if engine == "S":
                nc.scalar.copy(out=dst, in_=src)
            else:
                nc.vector.tensor_copy(out=dst, in_=src)

        def widen(engine, dst, src, scale):
            if engine == "S":
                nc.scalar.activation(out=dst, in_=src.bitcast(FP8), func=ACT.Copy, scale=scale)
            else:
                nc.vector.tensor_scalar(out=dst, in0=src.bitcast(FP8), scalar1=scale, scalar2=None, op0=ALU.mult)

        def widen_z(kg, h, who):
            dst = planes_of(("z", kg, h))
            width = 4 * UNIT // len(who)
            for i, engine in enumerate(who):
                t, lo = i % 4, i // 4 * width
                widen(engine, dst[:, t, lo:lo + width], z_bytes[kg, h][:, t, lo:lo + width], z_scale[:, kg, t:t + 1])

        def widen_a(pair, r, who):
            dst = planes_of(("a", pair, r))
            for i, engine in enumerate(who):
                t, g = i % 4, 2 * pair + i // 4
                lo = i // 4 * W
                widen(engine, dst[:, t, lo:lo + W], a_bytes[g][:, t, r * W:(r + 1) * W], a_scale[:, 4 * g + t:4 * g + t + 1])

        def mix(unit, who):
            dst, src = mixed_of(unit), planes[unit]
            width = UNIT // len(who)
            for i, engine in enumerate(who):
                lo = i * width
                piece = dst[:, lo:lo + width, :]
                if unit[0] == "z":
                    group, t0, tiles = lo // W * W, lo % W // P, width // P
                    by_tile = src[:, :, group:group + W].rearrange("p j (c i t) -> p t c j i", i=4, t=4)
                    copy(engine, piece.rearrange("p (t c i) j -> p t c j i", t=tiles, i=4), by_tile[:, t0:t0 + tiles])
                else:
                    columns = src[:, :, lo:lo + width].rearrange("p t (c i) -> p c t i", i=4)
                    copy(engine, piece.rearrange("p (c i) t -> p c t i", i=4), columns)

        def quantize(unit, part, parts):
            if unit not in codes:
                codes[unit] = keep.tile([P, UNIT], U32, name="codes_" + unit_name(unit), align_bytes=64)
                scales[unit] = keep.tile([P, UNIT], U8, name="scales_" + unit_name(unit), align_bytes=64)
            width = UNIT // parts
            cols = slice(part * width, (part + 1) * width)
            nc.vector.quantize_mx(
                out=codes[unit][:, cols].bitcast(FP8X4),
                scales=scales[unit][:, cols],
                in_=mixed[unit][:, cols, :].rearrange("p n t -> p (n t)"),
            )

        free_banks = list(range(BANKS))

        def take_bank(name):
            index = free_banks.pop(0)
            return index, psum.tile([P, W], F32, tag=f"bank{index}", name=name)

        x_banks = {}

        def turn_x(h, kg):
            words = x_rows[h][:].rearrange("p b d -> p (b d)").bitcast(F32).rearrange("p (b w) -> p b w", b=HALF_QB)
            for pair in range(2):
                x_banks[h, kg, pair] = take_bank(f"x_turned_{h}_{kg}_{pair}")
                turned = x_banks[h, kg, pair][1][:].rearrange("p (u q) -> p u q", u=2)
                for b in range(2):
                    for u in range(2):
                        nc.tensor.transpose(
                            turned[:, u, b * P:(b + 1) * P],
                            words[:, 2 * pair + b, W // 2 * kg + u:W // 2 * (kg + 1):2],
                            identity[:],
                        )

        def copy_x(h, kg, who):
            dst = mixed_of(("x", h, 0))[:].rearrange("p n e -> p (n e)").bitcast(F32).rearrange("p (q u) -> p q u", u=2)
            for pair, engine in enumerate(who):
                index, bank = x_banks[h, kg, pair]
                lo = kg * W + pair * 2 * P
                copy(engine, dst[:, lo:lo + 2 * P, :], bank[:].rearrange("p (u q) -> p q u", u=2))
                free_banks.append(index)

        def product(sums, left, left_cols, right, right_cols, start, stop):
            nc.tensor.matmul_mx(
                out=sums,
                lhsT=codes[left][:, left_cols].bitcast(FP8X4),
                lhsT_scale=scales[left][:, left_cols],
                rhs=codes[right][:, right_cols].bitcast(FP8X4),
                rhs_scale=scales[right][:, right_cols],
                start=start,
                stop=stop,
            )

        def place(c, g):
            width = CHUNKS[c][1] * P
            return ("e", c, g * width // UNIT), g * width % UNIT, width

        def stage1(c, g):
            unit, lo, width = place(c, g)
            dst = planes_of(unit)
            z_lo = g % 2 * W
            half, first = CHUNKS[c][0] // HALF_QB, CHUNKS[c][0] % HALF_QB * P
            tiles = {}
            for t in range(5):
                if t < 4:
                    tiles[t] = take_bank(f"s_{c}_{g}_{t}")
                    for kg in range(KG):
                        product(
                            tiles[t][1][:, :width],
                            ("z", kg, g // 2), slice(z_lo + t * P, z_lo + (t + 1) * P),
                            ("x", half, 0), slice(kg * W + first, kg * W + first + width),
                            kg == 0, kg == KG - 1,
                        )
                if t > 0:
                    index, bank = tiles[t - 1]
                    column = 4 * g + t - 1
                    nc.scalar.activation(
                        out=dst[:, t - 1, lo:lo + width], in_=bank[:, :width], func=ACT.Exp, bias=ln_az[:, column:column + 1]
                    )
                    free_banks.append(index)

        out_banks = {}

        def stage2(b, r, groups):
            if (b, r) not in out_banks:
                out_banks[b, r] = take_bank(f"p_{b}_{r}")
            c = [i for i, (first, count) in enumerate(CHUNKS) if first <= b < first + count][0]
            for g in groups:
                unit, lo = place(c, g)[:2]
                e_lo = lo + (b - CHUNKS[c][0]) * P
                a_lo = g % 2 * W
                product(
                    out_banks[b, r][1][:], unit, slice(e_lo, e_lo + P), ("a", g // 2, r), slice(a_lo, a_lo + W), g == 0, g == NG - 1
                )

        out_rows = out.rearrange("(p b) r -> p b r", b=QB)

        def finish(b, r):
            index, bank = out_banks[b, r]
            row = rows.tile([P, W], F32, tag="row", name=f"row_{b}_{r}")
            cols = slice(r * W, (r + 1) * W)
            nc.vector.scalar_tensor_tensor(
                out=row[:], in0=bank[:], scalar=ax_in[:, b:b + 1], in1=offset_in[:, cols], op0=ALU.mult, op1=ALU.add
            )
            free_banks.append(index)
            nc.sync.dma_start(out=out_rows[:, b, cols], in_=row[:])

        turn_x(0, 0)
        turn_x(0, 1)
        take_logs()
        add_logs()
        widen_z(0, 0, "SVVSVVVV")
        widen_z(1, 0, "SSVSVSSV")
        mix(("z", 1, 0), "VV")
        turn_x(1, 0)
        mix(("z", 0, 0), "VVVS")
        widen_z(0, 1, "SVSSSVSV")
        copy_x(0, 1, "SS")
        quantize(("z", 0, 0), 0, 1)
        copy_x(0, 0, "SS")
        turn_x(1, 1)
        quantize(("x", 0, 0), 0, 1)
        quantize(("z", 1, 0), 0, 1)
        mix(("z", 0, 1), "VVVS")
        copy_x(1, 0, "SS")
        copy_x(1, 1, "SS")
        quantize(("x", 1, 0), 0, 1)
        widen_z(1, 1, "VVVS")
        sign_a_scale()
        stage1(0, 0)
        mix(("z", 1, 1), "VS")
        quantize(("z", 0, 1), 0, 1)
        widen_a(0, 0, "VVVVVVSV")
        stage1(0, 1)
        stage1(2, 1)
        quantize(("z", 1, 1), 0, 1)
        mix(("a", 0, 0), "V")
        stage1(1, 1)
        stage1(2, 3)
        stage1(1, 3)
        mix(("e", 0, 0), "V")
        stage1(0, 3)
        quantize(("a", 0, 0), 0, 1)
        quantize(("e", 0, 0), 0, 1)
        widen_a(0, 1, "VVSVVVSS")
        widen_a(1, 1, "SVVSVSVV")
        mix(("a", 0, 1), "SVVV")
        stage1(0, 2)
        stage2(3, 0, (0,))
        mix(("a", 1, 1), "V")
        stage2(3, 0, (1,))
        stage2(2, 0, (0,))
        quantize(("a", 0, 1), 0, 1)
        quantize(("a", 1, 1), 0, 1)
        stage2(0, 0, (0,))
        stage2(1, 0, (0,))
        stage2(1, 0, (1,))
        stage2(2, 0, (1,))
        stage2(0, 0, (1,))
        stage1(1, 2)
        stage1(1, 0)
        stage1(2, 2)
        stage1(2, 0)
        stage2(3, 1, (0,))
        stage2(3, 1, (1,))
        mix(("e", 0, 1), "V")
        stage2(2, 1, (0,))
        widen_a(1, 0, "SVVSVSSS")
        stage2(1, 1, (0,))
        quantize(("e", 0, 1), 0, 1)
        stage2(0, 1, (0,))
        stage2(1, 1, (1,))
        stage2(2, 1, (1,))
        stage2(0, 1, (1,))
        mix(("a", 1, 0), "VVVS")
        stage2(3, 1, (2,))
        stage2(3, 1, (3,))
        quantize(("a", 1, 0), 0, 2)
        stage2(2, 1, (2,))
        stage2(1, 1, (2,))
        mix(("e", 2, 0), "VSSS")
        quantize(("a", 1, 0), 1, 2)
        stage2(2, 1, (3,))
        stage2(0, 1, (2,))
        quantize(("e", 2, 0), 0, 4)
        stage2(0, 1, (3,))
        finish(3, 1)
        stage2(1, 1, (3,))
        quantize(("e", 2, 0), 1, 4)
        finish(2, 1)
        stage2(0, 0, (2,))
        stage2(1, 0, (2,))
        stage2(3, 0, (2,))
        stage2(2, 0, (2,))
        finish(1, 1)
        mix(("e", 1, 0), "SS")
        stage2(2, 0, (3,))
        stage2(1, 0, (3,))
        quantize(("e", 2, 0), 2, 4)
        stage2(0, 0, (3,))
        stage2(3, 0, (3,))
        stage2(6, 0, (0,))
        stage2(6, 0, (1,))
        finish(1, 0)
        stage2(7, 0, (0,))
        stage2(7, 0, (1,))
        stage2(7, 1, (0,))
        quantize(("e", 2, 0), 3, 4)
        finish(2, 0)
        stage2(7, 1, (1,))
        stage2(6, 0, (2,))
        stage2(7, 1, (2,))
        stage2(6, 1, (0,))
        stage2(6, 1, (1,))
        finish(3, 0)
        finish(0, 1)
        stage2(7, 0, (2,))
        stage2(7, 0, (3,))
        quantize(("e", 1, 0), 0, 2)
        finish(7, 0)
        finish(0, 0)
        stage2(6, 1, (2,))
        stage2(7, 1, (3,))
        stage2(6, 0, (3,))
        stage2(6, 1, (3,))
        stage2(4, 1, (0,))
        stage2(4, 0, (0,))
        stage2(4, 0, (1,))
        stage2(5, 0, (0,))
        stage2(4, 1, (1,))
        finish(6, 0)
        quantize(("e", 1, 0), 1, 2)
        stage2(5, 0, (1,))
        stage2(5, 1, (0,))
        stage2(5, 1, (1,))
        finish(7, 1)
        stage2(4, 0, (2,))
        finish(6, 1)
        stage2(4, 0, (3,))
        finish(4, 0)
        stage2(4, 1, (2,))
        stage2(5, 0, (2,))
        stage2(4, 1, (3,))
        finish(4, 1)
        stage2(5, 1, (2,))
        stage2(5, 0, (3,))
        finish(5, 0)
        stage2(5, 1, (3,))
        finish(5, 1)
